import numpy as np
import ml_dtypes


def mxq(x, axis, fmt="e4m3"):
    dtype, down = {"e4m3": (ml_dtypes.float8_e4m3fn, 7), "e5m2": (ml_dtypes.float8_e5m2, 14)}[fmt]
    v = np.moveaxis(np.asarray(x, np.float32).astype(ml_dtypes.bfloat16).astype(np.float64), axis, -1)
    blocks = v.reshape(v.shape[:-1] + (-1, 32))
    amax = np.abs(blocks).max(-1, keepdims=True)
    byte = np.maximum(np.where(amax > 0, np.frexp(amax)[1] - 1 + 127, 0) - down, 1)
    scale = np.exp2(byte - 127.0)
    codes = (blocks / scale).astype(np.float32).astype(dtype).astype(np.float64)
    return np.moveaxis((codes * scale).reshape(v.shape), -1, axis)


WIDE = False


def mx_kscale(k):
    if not WIDE:
        return np.ones(k)
    levels = np.array([10, -10, 5, -5, 0])
    if k % 512:
        return np.exp2(np.random.permutation(np.resize(levels, k // 32))).repeat(32)
    a = np.empty((k // 512, 16))
    for p in range(k // 512):
        a[p, :8] = np.random.permutation(np.resize(levels, 8))
        for g in range(8):
            far = levels[np.abs(levels - a[p, g]) >= 10]
            a[p, g + 8] = far[np.random.randint(len(far))]
    return np.exp2(a.ravel()).repeat(32)


def f64(x):
    return np.asarray(x).astype(np.float64)


def striped(idx):
    return np.tile(idx.reshape(-1, 16).T, (8, 1)).astype(np.uint16)


def unstriped(offs):
    return offs[:16].T.reshape(-1).astype(np.int64)


E2M1 = np.array([0.0, 0.5, 1.0, 1.5, 2.0, 3.0, 4.0, 6.0, -0.0, -0.5, -1.0, -1.5, -2.0, -3.0, -4.0, -6.0])


def pack_weight(w, fmt):
    k, n = w.shape
    w = f64(np.asarray(w, np.float32).astype(ml_dtypes.bfloat16)).reshape(k // 32, 32, n)
    amax = np.abs(w).max(1)
    if fmt == "e4m3":
        byte = np.frexp(amax)[1] - 1 + 127 - 7
    else:
        mant, ex = np.frexp(amax / 6.0)
        byte = np.where(mant > 0.5, ex, ex - 1) + 127
    byte = np.clip(np.where(amax > 0, byte, 1), 1, 254)
    scaled = (w * np.exp2(127.0 - byte)[:, None, :]).reshape(k, n).astype(np.float32)
    by_word = np.ascontiguousarray(scaled.reshape(k // 512, 128, 4, n).transpose(0, 1, 3, 2))
    if fmt == "e4m3":
        words = by_word.astype(ml_dtypes.float8_e4m3fn).view(np.uint8)
    else:
        c = by_word.astype(ml_dtypes.float4_e2m1fn).view(np.uint8) & 0xF
        words = (c[..., 0::2] | (c[..., 1::2] << 4)).reshape(k // 512, 128, 2 * n)
    return np.ascontiguousarray(words), np.ascontiguousarray(byte.astype(np.uint8).reshape(k // 512, 16, n))


def unpack_weight(words, scales, fmt):
    g, _, n = scales.shape
    words = np.ascontiguousarray(words).reshape(g, 128, n, -1)
    if fmt == "e4m3":
        vals = words.view(ml_dtypes.float8_e4m3fn).astype(np.float64)
    else:
        nib = np.empty((g, 128, n, 4), np.uint8)
        nib[..., 0::2] = words & 0xF
        nib[..., 1::2] = words >> 4
        vals = E2M1[nib]
    vals = vals * np.repeat(np.exp2(scales.astype(np.float64) - 127.0), 8, axis=1)[..., None]
    return vals.transpose(0, 1, 3, 2).reshape(g * 512, n)


def gelu(v):
    return 0.5 * v * (1.0 + np.tanh(np.sqrt(2.0 / np.pi) * (v + 0.044715 * v**3)))


K, K2, H, N, T, S, P, T2 = 1024, 512, 1024, 512, 2048, 1024, 512, 2048

def setup_inputs():
    n = np.random.standard_normal
    s, s2, u = mx_kscale(K)[:, None], mx_kscale(K2)[:, None], mx_kscale(H)[:, None]
    tab_words, tab_scales = pack_weight(n((K, T)) * s, "e4m3")
    tab2_words, tab2_scales = pack_weight(n((K2, T)) * s2, "e4m3")
    w2_words, w2_scales = pack_weight(n((K2, H)) / s2 / np.sqrt(K2), "e2m1")
    w4_words, w4_scales = pack_weight(n((H, N)) / u / np.sqrt(H), "e4m3")
    perm = np.random.permutation(T2)
    return {
        "tab_words": tab_words, "tab_scales": tab_scales,
        "tab2_words": tab2_words, "tab2_scales": tab2_scales,
        "offs": striped(np.random.permutation(T)[:S]),
        "offs2": striped(np.random.permutation(T)[:P]),
        "pos1": striped(np.random.permutation(S)[:P]),
        "offs3": striped(perm[:S]), "offs4": striped(perm[S:S + P]),
        "w1": (n((K, H)) / s / np.sqrt(K)).astype(np.float32),
        "w2_words": w2_words, "w2_scales": w2_scales,
        "base": (0.8 * n((H, S))).astype(np.float32),
        "gain1": (1.3 * np.exp(0.3 * n(H)) * u[:, 0]).astype(np.float32),
        "gain2": (np.exp(0.3 * n(H)) * u[:, 0]).astype(np.float32),
        "w3": (n((H, N)) / u / np.sqrt(H)).astype(np.float32),
        "w4_words": w4_words, "w4_scales": w4_scales,
        "page1": n((N, T2)).astype(np.float32),
        "wg1": np.exp(0.3 * n((128, S))).astype(np.float32),
        "wg2": np.exp(0.3 * n((128, P))).astype(np.float32)}

def reference(tab_words, tab_scales, tab2_words, tab2_scales, offs, offs2, pos1, offs3, offs4, w1, w2_words, w2_scales, base, gain1, gain2, w3, w4_words, w4_scales, page1, wg1, wg2):
    v = unpack_weight(tab_words, tab_scales, "e4m3")[:, unstriped(offs)]
    v2 = unpack_weight(tab2_words, tab2_scales, "e4m3")[:, unstriped(offs2)]
    h1 = mxq(f64(w1), 0, "e4m3").T @ v
    h2 = unpack_weight(w2_words, w2_scales, "e2m1").T @ v2
    z1 = np.tanh(h1 + f64(base)) * f64(gain1)[:, None]
    z2 = np.minimum(h2, h1[:, unstriped(pos1)]) * f64(gain2)[:, None]
    y1 = mxq(f64(w3), 0, "e4m3").T @ mxq(z1, 0, "e4m3")
    y2 = unpack_weight(w4_words, w4_scales, "e4m3").T @ mxq(z2, 0, "e4m3")
    out = f64(page1).copy()
    out[:, unstriped(offs3)] = np.tile(f64(wg1), (N // 128, 1)) * y1
    out[:, unstriped(offs4)] = np.tile(f64(wg2), (N // 128, 1)) * y2
    return out

@@ -1,0 +1,317 @@
+from contextlib import ExitStack
+
+import concourse.mybir as mybir
+from concourse.masks import make_identity
+
+F32 = mybir.dt.float32
+BF16 = mybir.dt.bfloat16
+I32 = mybir.dt.int32
+U32 = mybir.dt.uint32
+U16 = mybir.dt.uint16
+U8 = mybir.dt.uint8
+FP8X4 = mybir.dt.float8_e4m3fn_x4
+FP4X4 = mybir.dt.float4_e2m1fn_x4
+ALU = mybir.AluOpType
+ACT = mybir.ActivationFunctionType
+
+K, K2, H, N, T, S, PF, T2 = 1024, 512, 1024, 512, 2048, 1024, 512, 2048
+P = 128
+PACK = 4
+PASS = P * PACK
+CH = 256
+FLOPS = 2 * (K * H * S + K2 * H * PF + H * N * S + H * N * PF)
+
+VECTOR_WEAVES = ()
+
+
+def tile_list_hull_fleet_page_kernel(
+    tc, tab_words, tab_scales, tab2_words, tab2_scales, offs, offs2, pos1, offs3, offs4,
+    w1, w2_words, w2_scales, base, gain1, gain2, w3, w4_words, w4_scales, page1, wg1, wg2, out,
+):
+    nc = tc.nc
+    with ExitStack() as ctx:
+        lists = ctx.enter_context(tc.tile_pool(name="lists", bufs=1))
+        keep = ctx.enter_context(tc.tile_pool(name="keep", bufs=1))
+        raw = ctx.enter_context(tc.tile_pool(name="raw", bufs=5))
+        work = ctx.enter_context(tc.tile_pool(name="work", bufs=2))
+        psum = ctx.enter_context(tc.psum_pool(name="psum", bufs=1))
+        banks = [psum.tile([P, PASS], F32, name="bank%d" % i) for i in range(8)]
+
+        def load_list(src, name):
+            tile = lists.tile([P, src.shape[1]], U16, name=name)
+            nc.sync.dma_start(tile[:], src)
+            return tile
+
+        def zeroed_plane(width, name):
+            plane = keep.tile([P, width], U8, name=name, align_bytes=64)
+            nc.vector.memset(plane[:].bitcast(I32), 0)
+            return plane
+
+        def load_plane(plane, scales, queue):
+            rows = 4 * scales.shape[0]
+            for q in range(4):
+                queue.dma_start(
+                    plane[32 * q : 32 * q + rows, :].bitcast(I32),
+                    scales[:, 4 * q : 4 * q + 4, :].bitcast(I32),
+                )
+
+        def load_words(words, name):
+            tile = keep.tile([P, words.shape[1]], I32, name=name, align_bytes=64)
+            nc.sync.dma_start(tile[:], words.rearrange("p c i -> p (c i)").bitcast(I32))
+            return tile
+
+        def load_rows(src, row0, col0, name):
+            tile = raw.tile([P, PACK, PASS], F32, name=name, tag="raw")
+            rows = src[row0 : row0 + PASS, col0 : col0 + PASS]
+            nc.sync.dma_start(tile[:], rows.rearrange("(p i) c -> p i c", i=PACK))
+            return tile
+
+        def load_gain(src, name):
+            tile = keep.tile([P, 2, PACK], F32, name=name)
+            nc.sync.dma_start(tile[:], src.rearrange("(b p t) -> p b t", p=P, t=PACK))
+            return tile
+
+        def load_plain(src, name):
+            tile = keep.tile([P, src.shape[1]], F32, name=name)
+            nc.sync.dma_start(tile[:], src)
+            return tile
+
+        tab_plane = zeroed_plane(T, "tab_plane")
+        w2_plane_in = zeroed_plane(H, "w2_plane_in")
+        tab2_plane = zeroed_plane(T, "tab2_plane")
+        w4_plane = zeroed_plane(N, "w4_plane")
+        ident = keep.tile([P, P], F32, name="ident")
+        make_identity(nc, ident[:])
+
+        idx = load_list(offs, "idx")
+        tab_w = [load_words(tab_words[0], "tab_w0")]
+        load_plane(tab_plane, tab_scales, nc.sync)
+        tab_w.append(load_words(tab_words[1], "tab_w1"))
+        w2_in = keep.tile([P, 2 * H], U8, name="w2_in", align_bytes=64)
+        nc.sync.dma_start(w2_in[:].bitcast(I32), w2_words[0].bitcast(I32))
+        w1_raw = {(0, 0): load_rows(w1, 0, 0, "w1_00")}
+        w1_raw[1, 0] = load_rows(w1, PASS, 0, "w1_10")
+        idx2 = load_list(offs2, "idx2")
+        tab2_w = load_words(tab2_words[0], "tab2_w")
+        load_plane(tab2_plane, tab2_scales, nc.sync)
+        oldest = load_list(pos1, "oldest")
+        w1_raw[0, 1] = load_rows(w1, 0, PASS, "w1_01")
+        load_plane(w2_plane_in, w2_scales, nc.sync)
+        w1_raw[1, 1] = load_rows(w1, PASS, PASS, "w1_11")
+        g2 = load_gain(gain2, "g2")
+        g1 = load_gain(gain1, "g1")
+        base_sb = {(b, 0): load_rows(base, PASS * b, 0, "base_%d0" % b) for b in range(2)}
+        w3_raw = [load_rows(w3, PASS * b, 0, "w3_%d" % b) for b in range(2)]
+        w4_w = [load_words(w4_words[a], "w4_w%d" % a) for a in range(2)]
+        load_plane(w4_plane, w4_scales, nc.sync)
+        idx4 = load_list(offs4, "idx4")
+        wg2_sb = load_plain(wg2, "wg2_sb")
+        pages = [load_plain(page1[n * P : (n + 1) * P, :], "page%d" % n) for n in range(4)]
+        idx3 = load_list(offs3, "idx3")
+        wg1_sb = load_plain(wg1, "wg1_sb")
+        for b in range(2):
+            base_sb[b, 1] = load_rows(base, PASS * b, PASS, "base_%d1" % b)
+
+        def gather(window, offsets, dtype, name):
+            count = 16 * offsets.shape[1]
+            picked = keep.tile([P, count], dtype, name=name, align_bytes=64)
+            nc.vector.tensor_copy(picked[:], window.indirect(offsets[:]))
+            return picked
+
+        def quantise(src, pool, name, bufs):
+            width = src.shape[1] // PACK
+            codes = pool.tile([P, width], U32, name=name + "_codes", bufs=bufs, align_bytes=64)
+            plane = pool.tile([P, width], U8, name=name + "_plane", bufs=bufs, align_bytes=64)
+            nc.vector.quantize_mx(out=codes[:].bitcast(FP8X4), scales=plane[:], in_=src)
+            return codes, plane
+
+        def round_w1(a, b):
+            wb = work.tile([P, PASS * PACK], BF16, name="wb", tag="wb", align_bytes=64)
+            dst = wb[:].rearrange("p (t m i) -> p m t i", t=PACK, i=PACK)
+            src = w1_raw[a, b][:].rearrange("p i (m t) -> p m t i", t=PACK)
+            if (a, b) not in ((1, 0), (1, 1)):
+                nc.scalar.copy(dst, src)
+            else:
+                nc.vector.tensor_copy(dst, src)
+            return quantise(wb[:], keep, "w1q%d%d" % (a, b), 1)
+
+        def round_w3(b):
+            wb = work.tile([P, PASS * PACK], BF16, name="wb", tag="wb", align_bytes=64)
+            nc.vector.tensor_copy(
+                wb[:].rearrange("p (c e i) -> p c i e", e=4, i=PACK),
+                w3_raw[b][:].rearrange("p i (c e) -> p c i e", e=4),
+            )
+            return quantise(wb[:], keep, "w3q%d" % b, 1)
+
+        v_w = [gather(tab_w[0][:].bitcast(U32), idx, U32, "v_w0")]
+        v_plane = gather(tab_plane[:], idx, U8, "v_plane")
+        v_w.append(gather(tab_w[1][:].bitcast(U32), idx, U32, "v_w1"))
+
+        w2_w = keep.tile([P, 2 * H], U8, name="w2_w", align_bytes=64)
+        nc.vector.tensor_copy(
+            w2_w[:].bitcast(U16).rearrange("p (b t m) -> p b t m", b=2, t=PACK),
+            w2_in[:].bitcast(U16).rearrange("p (b m t) -> p b t m", b=2, t=PACK),
+        )
+        w2_plane = keep.tile([P, H], U8, name="w2_plane", align_bytes=64)
+        nc.vector.tensor_copy(
+            w2_plane[:].rearrange("p (b t m) -> p b t m", b=2, t=PACK),
+            w2_plane_in[:].rearrange("p (b m t) -> p b t m", b=2, t=PACK),
+        )
+
+        h1 = {}
+
+        def make_h1(b, w1q):
+            for t in range(PACK):
+                rows = keep.tile([P, S], F32, name="h1_%d%d" % (b, t))
+                h1[b, t] = rows
+                mcols = slice(P * t, P * (t + 1))
+                for jh in range(2):
+                    jcols = slice(PASS * jh, PASS * (jh + 1))
+                    bank = banks[(2 * t + jh) % 3]
+                    for a in range(2):
+                        codes, plane = w1q[a]
+                        nc.tensor.matmul_mx(
+                            out=bank[:],
+                            lhsT=codes[:, mcols].bitcast(FP8X4),
+                            lhsT_scale=plane[:, mcols],
+                            rhs=v_w[a][:, jcols].bitcast(FP8X4),
+                            rhs_scale=v_plane[4 * a : P, jcols],
+                            start=(a == 0),
+                            stop=(a == 1),
+                        )
+                    nc.scalar.copy(rows[:, jcols], bank[:])
+
+        def new_z():
+            return work.tile([P, 2, CH, PACK], BF16, name="zb", tag="zb", align_bytes=64)
+
+        def weave(copy, zb, b, planes):
+            copy(
+                zb[:, b].rearrange("p (c e) t -> p c t e", e=4),
+                planes.rearrange("p t (c e) -> p c t e", e=4),
+            )
+
+        def fleet_planes(b):
+            planes = work.tile([P, PACK, PF], BF16, name="fplanes", tag="planes")
+            for t in range(PACK):
+                picked = work.tile([P, PF], F32, name="picked", tag="picked")
+                nc.vector.tensor_copy(picked[:], h1[b, t][:].indirect(oldest[:]))
+                bank = banks[3 + t % 2]
+                col = PASS * b + P * t
+                nc.tensor.matmul_mx(
+                    out=bank[:],
+                    lhsT=w2_w[:, 2 * col : 2 * (col + P)].bitcast(FP4X4),
+                    lhsT_scale=w2_plane[:, col : col + P],
+                    rhs=v2_w[:].bitcast(FP8X4),
+                    rhs_scale=v2_plane[:],
+                    start=True,
+                    stop=True,
+                )
+                least = work.tile([P, PF], F32, name="least", tag="least", bufs=4)
+                nc.vector.tensor_tensor(least[:], bank[:], picked[:], ALU.min)
+                nc.scalar.activation(planes[:, t, :], least[:], ACT.Copy, scale=g2[:, b, t : t + 1])
+            return planes
+
+        def vessel_tanh(b, j0):
+            bank = banks[5 + (j0 // P) % 2][:].rearrange("p (t j) -> p t j", t=PACK)
+            given = base_sb[b, j0 // PASS]
+            jj = j0 % PASS
+            for t in range(PACK):
+                nc.tensor.matmul(bank[:, t, :], lhsT=h1[b, t][:, j0 : j0 + P], rhs=ident[:],
+                                 start=True, stop=False, is_transpose=True)
+                nc.tensor.matmul(bank[:, t, :], lhsT=given[:, t, jj : jj + P], rhs=ident[:],
+                                 start=False, stop=True, is_transpose=True)
+            th = work.tile([P, PACK, P], F32, name="th", tag="th", bufs=4)
+            nc.scalar.activation(th[:], bank, ACT.Tanh)
+            return th
+
+        def vessel_half(zb, c, b):
+            ths = [vessel_tanh(b, CH * c + P * s) for s in range(2)]
+            planes = work.tile([P, PACK, CH], BF16, name="planes", tag="planes")
+            for u in range(2):
+                bank = banks[2 * b + u][:].rearrange("p (e j) -> p e j", e=2)
+                for e in range(2):
+                    for s in range(2):
+                        nc.tensor.transpose(bank[:, e, P * s : P * (s + 1)], ths[s][:, 2 * u + e, :], ident[:])
+                for e in range(2):
+                    t = 2 * u + e
+                    nc.scalar.activation(planes[:, t, :], bank[:, e, :], ACT.Copy, scale=g1[:, b, t : t + 1])
+            weave(nc.vector.tensor_copy if (c, b) in VECTOR_WEAVES else nc.scalar.copy, zb, b, planes[:])
+
+        def quantise_z(zb):
+            return quantise(zb[:].rearrange("p b j t -> p (b j t)"), work, "zq", 3)
+
+        def product(bank, weights, parts):
+            for e, (n, (codes, plane)) in enumerate(parts):
+                ncols = slice(P * n, P * (n + 1))
+                for b in range(2):
+                    wcodes, wplane = weights[b]
+                    nc.tensor.matmul_mx(
+                        out=bank[:, CH * e : CH * (e + 1)],
+                        lhsT=wcodes[:, ncols].bitcast(FP8X4),
+                        lhsT_scale=wplane[:, ncols],
+                        rhs=codes[:, CH * b : CH * (b + 1)].bitcast(FP8X4),
+                        rhs_scale=plane[:, CH * b : CH * (b + 1)],
+                        start=(b == 0),
+                        stop=(b == 1),
+                    )
+            y = work.tile([P, 2 * CH], F32, name="y", tag="y", bufs=4)
+            nc.scalar.copy(y[:, 0 : CH * len(parts)], bank[:, 0 : CH * len(parts)])
+            return y
+
+        def scatter(n, values, offsets, factors, j0, count):
+            nc.vector.tensor_tensor(
+                pages[n][:].indirect(offsets[:, j0 // 16 : (j0 + count) // 16]),
+                values,
+                factors[:, j0 : j0 + count],
+                ALU.mult,
+            )
+
+        def place_pair(bank, weights, zq, offsets, factors, c, u):
+            y = product(bank, weights, [(2 * u, zq), (2 * u + 1, zq)])
+            for e in range(2):
+                scatter(2 * u + e, y[:, CH * e : CH * (e + 1)], offsets, factors, CH * c, CH)
+
+        def store(n):
+            nc.sync.dma_start(out[P * n : P * (n + 1), :], pages[n][:])
+
+        w1q0 = [round_w1(0, 0), round_w1(1, 0)]
+        v2_w = gather(tab2_w[:].bitcast(U32), idx2, U32, "v2_w")
+        v2_plane = gather(tab2_plane[:], idx2, U8, "v2_plane")
+        make_h1(0, w1q0)
+        w1q1 = [round_w1(0, 1), round_w1(1, 1)]
+        make_h1(1, w1q1)
+        zf = [new_z() for c in range(2)]
+        w4q = [(w4_w[a], w4_plane[4 * a : P, :]) for a in range(2)]
+        for b in range(2):
+            planes = fleet_planes(b)
+            if b == 0:
+                for c in range(2):
+                    weave(nc.scalar.copy, zf[c], b, planes[:, :, CH * c : CH * (c + 1)])
+        w3q = [round_w3(b) for b in range(2)]
+        weave(nc.scalar.copy, zf[0], 1, planes[:, :, 0:CH])
+        chunks = [(w4q, quantise_z(zf[0]), idx4, wg2_sb, 0)]
+        place_pair(banks[7], *chunks[0], 0)
+        weave(nc.scalar.copy, zf[1], 1, planes[:, :, CH : 2 * CH])
+        chunks.append((w4q, quantise_z(zf[1]), idx4, wg2_sb, 1))
+        place_pair(banks[4], *chunks[0], 1)
+        for c in range(4):
+            zb = new_z()
+            vessel_half(zb, c, 0)
+            place_pair(banks[1], *chunks[-1], 0)
+            vessel_half(zb, c, 1)
+            zq = quantise_z(zb)
+            if c < 3:
+                place_pair(banks[3], *chunks[-1], 1)
+            chunks.append((w3q, zq, idx3, wg1_sb, c))
+        before, last = chunks[-2][1], chunks[-1][1]
+        y = product(banks[3], w3q, [(2, before)])
+        scatter(2, y[:, 0:CH], idx3, wg1_sb, 2 * CH, CH)
+        place_pair(banks[7], *chunks[-1], 0)
+        store(0)
+        store(1)
+        y = product(banks[4], w3q, [(2, last)])
+        scatter(2, y[:, 0:CH], idx3, wg1_sb, 3 * CH, CH)
+        store(2)
+        y = product(banks[5], w3q, [(3, before), (3, last)])
+        scatter(3, y[:], idx3, wg1_sb, 2 * CH, 2 * CH)
+        store(3)

@@ -21,7 +21,9 @@ PASS = P * PACK
 CH = 256
 FLOPS = 2 * (K * H * S + K2 * H * PF + H * N * S + H * N * PF)
 
-VECTOR_WEAVES = ()
+H2_BANKS = ((3, 4, 0, 1), (2, 3, 4, 7))
+AHEAD = 4
+H1_ON = {(0, 0): "rows01", (0, 1): "rows00", (1, 0): "rows10", (1, 1): "rows11"}
 
 
 def tile_list_hull_fleet_page_kernel(
@@ -32,7 +34,6 @@ def tile_list_hull_fleet_page_kernel(
     with ExitStack() as ctx:
         lists = ctx.enter_context(tc.tile_pool(name="lists", bufs=1))
         keep = ctx.enter_context(tc.tile_pool(name="keep", bufs=1))
-        raw = ctx.enter_context(tc.tile_pool(name="raw", bufs=5))
         work = ctx.enter_context(tc.tile_pool(name="work", bufs=2))
         psum = ctx.enter_context(tc.psum_pool(name="psum", bufs=1))
         banks = [psum.tile([P, PASS], F32, name="bank%d" % i) for i in range(8)]
@@ -47,10 +48,10 @@ def tile_list_hull_fleet_page_kernel(
             nc.vector.memset(plane[:].bitcast(I32), 0)
             return plane
 
-        def load_plane(plane, scales, queue):
+        def load_plane(plane, scales):
             rows = 4 * scales.shape[0]
             for q in range(4):
-                queue.dma_start(
+                nc.sync.dma_start(
                     plane[32 * q : 32 * q + rows, :].bitcast(I32),
                     scales[:, 4 * q : 4 * q + 4, :].bitcast(I32),
                 )
@@ -61,7 +62,7 @@ def tile_list_hull_fleet_page_kernel(
             return tile
 
         def load_rows(src, row0, col0, name):
-            tile = raw.tile([P, PACK, PASS], F32, name=name, tag="raw")
+            tile = keep.tile([P, PACK, PASS], F32, name=name)
             rows = src[row0 : row0 + PASS, col0 : col0 + PASS]
             nc.sync.dma_start(tile[:], rows.rearrange("(p i) c -> p i c", i=PACK))
             return tile
@@ -85,32 +86,33 @@ def tile_list_hull_fleet_page_kernel(
 
         idx = load_list(offs, "idx")
         tab_w = [load_words(tab_words[0], "tab_w0")]
-        load_plane(tab_plane, tab_scales, nc.sync)
+        load_plane(tab_plane, tab_scales)
         tab_w.append(load_words(tab_words[1], "tab_w1"))
         w2_in = keep.tile([P, 2 * H], U8, name="w2_in", align_bytes=64)
         nc.sync.dma_start(w2_in[:].bitcast(I32), w2_words[0].bitcast(I32))
-        w1_raw = {(0, 0): load_rows(w1, 0, 0, "w1_00")}
-        w1_raw[1, 0] = load_rows(w1, PASS, 0, "w1_10")
+        w1_raw = {(a, 0): load_rows(w1, PASS * a, 0, "rows%d0" % a) for a in range(2)}
+        load_plane(w2_plane_in, w2_scales)
+        for a in range(2):
+            w1_raw[a, 1] = load_rows(w1, PASS * a, PASS, "rows%d1" % a)
+        oldest = load_list(pos1, "oldest")
         idx2 = load_list(offs2, "idx2")
         tab2_w = load_words(tab2_words[0], "tab2_w")
-        load_plane(tab2_plane, tab2_scales, nc.sync)
-        oldest = load_list(pos1, "oldest")
-        w1_raw[0, 1] = load_rows(w1, 0, PASS, "w1_01")
-        load_plane(w2_plane_in, w2_scales, nc.sync)
-        w1_raw[1, 1] = load_rows(w1, PASS, PASS, "w1_11")
+        load_plane(tab2_plane, tab2_scales)
         g2 = load_gain(gain2, "g2")
         g1 = load_gain(gain1, "g1")
-        base_sb = {(b, 0): load_rows(base, PASS * b, 0, "base_%d0" % b) for b in range(2)}
-        w3_raw = [load_rows(w3, PASS * b, 0, "w3_%d" % b) for b in range(2)]
+        base_sb = {(0, 0): load_rows(base, 0, 0, "base0")}
+        base_sb[1, 0] = load_rows(base, PASS, 0, "base1")
+        w3_raw = [load_rows(w3, PASS * b, 0, "late%d" % b) for b in range(2)]
         w4_w = [load_words(w4_words[a], "w4_w%d" % a) for a in range(2)]
-        load_plane(w4_plane, w4_scales, nc.sync)
+        load_plane(w4_plane, w4_scales)
         idx4 = load_list(offs4, "idx4")
         wg2_sb = load_plain(wg2, "wg2_sb")
         pages = [load_plain(page1[n * P : (n + 1) * P, :], "page%d" % n) for n in range(4)]
         idx3 = load_list(offs3, "idx3")
         wg1_sb = load_plain(wg1, "wg1_sb")
-        for b in range(2):
-            base_sb[b, 1] = load_rows(base, PASS * b, PASS, "base_%d1" % b)
+
+        stage = [keep.tile([P, 2 * PF], F32, name="stage%d" % i, align_bytes=64) for i in range(2)]
+        planes = [keep.tile([P, PACK, PF], BF16, name="planes%d" % b) for b in range(2)]
 
         def gather(window, offsets, dtype, name):
             count = 16 * offsets.shape[1]
@@ -126,22 +128,22 @@ def tile_list_hull_fleet_page_kernel(
             return codes, plane
 
         def round_w1(a, b):
-            wb = work.tile([P, PASS * PACK], BF16, name="wb", tag="wb", align_bytes=64)
-            dst = wb[:].rearrange("p (t m i) -> p m t i", t=PACK, i=PACK)
+            wb = stage[a][:].bitcast(BF16)
+            dst = wb.rearrange("p (t m i) -> p m t i", t=PACK, i=PACK)
             src = w1_raw[a, b][:].rearrange("p i (m t) -> p m t i", t=PACK)
-            if (a, b) not in ((1, 0), (1, 1)):
+            if a == 0:
                 nc.scalar.copy(dst, src)
             else:
                 nc.vector.tensor_copy(dst, src)
-            return quantise(wb[:], keep, "w1q%d%d" % (a, b), 1)
+            return quantise(wb, keep, "w1q%d%d" % (a, b), 1)
 
         def round_w3(b):
-            wb = work.tile([P, PASS * PACK], BF16, name="wb", tag="wb", align_bytes=64)
+            wb = stage[b][:].bitcast(BF16)
             nc.vector.tensor_copy(
-                wb[:].rearrange("p (c e i) -> p c i e", e=4, i=PACK),
+                wb.rearrange("p (c e i) -> p c i e", e=4, i=PACK),
                 w3_raw[b][:].rearrange("p i (c e) -> p c i e", e=4),
             )
-            return quantise(wb[:], keep, "w3q%d" % b, 1)
+            return quantise(wb, keep, "w3q%d" % b, 1)
 
         v_w = [gather(tab_w[0][:].bitcast(U32), idx, U32, "v_w0")]
         v_plane = gather(tab_plane[:], idx, U8, "v_plane")
@@ -162,7 +164,9 @@ def tile_list_hull_fleet_page_kernel(
 
         def make_h1(b, w1q):
             for t in range(PACK):
-                rows = keep.tile([P, S], F32, name="h1_%d%d" % (b, t))
+                if t % 2 == 0:
+                    pair = keep.tile([P, 2, S], F32, name="h1_%d%d" % (b, t), tag=H1_ON[b, t // 2])
+                rows = pair[:, t % 2, :]
                 h1[b, t] = rows
                 mcols = slice(P * t, P * (t + 1))
                 for jh in range(2):
@@ -184,18 +188,17 @@ def tile_list_hull_fleet_page_kernel(
         def new_z():
             return work.tile([P, 2, CH, PACK], BF16, name="zb", tag="zb", align_bytes=64)
 
-        def weave(copy, zb, b, planes):
-            copy(
+        def weave(zb, b, rows):
+            nc.scalar.copy(
                 zb[:, b].rearrange("p (c e) t -> p c t e", e=4),
-                planes.rearrange("p t (c e) -> p c t e", e=4),
+                rows.rearrange("p t (c e) -> p c t e", e=4),
             )
 
         def fleet_planes(b):
-            planes = work.tile([P, PACK, PF], BF16, name="fplanes", tag="planes")
             for t in range(PACK):
-                picked = work.tile([P, PF], F32, name="picked", tag="picked")
-                nc.vector.tensor_copy(picked[:], h1[b, t][:].indirect(oldest[:]))
-                bank = banks[3 + t % 2]
+                picked = stage[t // 2][:, PF * (t % 2) : PF * (t % 2 + 1)]
+                nc.vector.tensor_copy(picked, h1[b, t].indirect(oldest[:]))
+                bank = banks[H2_BANKS[b][t]]
                 col = PASS * b + P * t
                 nc.tensor.matmul_mx(
                     out=bank[:],
@@ -207,9 +210,10 @@ def tile_list_hull_fleet_page_kernel(
                     stop=True,
                 )
                 least = work.tile([P, PF], F32, name="least", tag="least", bufs=4)
-                nc.vector.tensor_tensor(least[:], bank[:], picked[:], ALU.min)
-                nc.scalar.activation(planes[:, t, :], least[:], ACT.Copy, scale=g2[:, b, t : t + 1])
-            return planes
+                nc.vector.tensor_tensor(least[:], bank[:], picked, ALU.min)
+                nc.scalar.activation(planes[b][:, t, :], least[:], ACT.Copy, scale=g2[:, b, t : t + 1])
+                if len(tanhs) < AHEAD and True:
+                    vessel_ahead()
 
         def vessel_tanh(b, j0):
             bank = banks[5 + (j0 // P) % 2][:].rearrange("p (t j) -> p t j", t=PACK)
@@ -220,13 +224,20 @@ def tile_list_hull_fleet_page_kernel(
                                  start=True, stop=False, is_transpose=True)
                 nc.tensor.matmul(bank[:, t, :], lhsT=given[:, t, jj : jj + P], rhs=ident[:],
                                  start=False, stop=True, is_transpose=True)
-            th = work.tile([P, PACK, P], F32, name="th", tag="th", bufs=4)
+            th = work.tile([P, PACK, P], F32, name="th", tag="th", bufs=AHEAD + 2)
             nc.scalar.activation(th[:], bank, ACT.Tanh)
             return th
 
+        tanhs = []
+
+        def vessel_ahead():
+            k = len(tanhs)
+            if k < 16:
+                tanhs.append(vessel_tanh(k // 2 % 2, CH * (k // 4) + P * (k % 2)))
+
         def vessel_half(zb, c, b):
-            ths = [vessel_tanh(b, CH * c + P * s) for s in range(2)]
-            planes = work.tile([P, PACK, CH], BF16, name="planes", tag="planes")
+            ths = tanhs[4 * c + 2 * b : 4 * c + 2 * b + 2]
+            rounded = planes[b][:, :, CH * (c % 2) : CH * (c % 2 + 1)]
             for u in range(2):
                 bank = banks[2 * b + u][:].rearrange("p (e j) -> p e j", e=2)
                 for e in range(2):
@@ -234,8 +245,10 @@ def tile_list_hull_fleet_page_kernel(
                         nc.tensor.transpose(bank[:, e, P * s : P * (s + 1)], ths[s][:, 2 * u + e, :], ident[:])
                 for e in range(2):
                     t = 2 * u + e
-                    nc.scalar.activation(planes[:, t, :], bank[:, e, :], ACT.Copy, scale=g1[:, b, t : t + 1])
-            weave(nc.vector.tensor_copy if (c, b) in VECTOR_WEAVES else nc.scalar.copy, zb, b, planes[:])
+                    nc.scalar.activation(rounded[:, t, :], bank[:, e, :], ACT.Copy, scale=g1[:, b, t : t + 1])
+            vessel_ahead()
+            weave(zb, b, rounded)
+            vessel_ahead()
 
         def quantise_z(zb):
             return quantise(zb[:].rearrange("p b j t -> p (b j t)"), work, "zq", 3)
@@ -274,24 +287,24 @@ def tile_list_hull_fleet_page_kernel(
         def store(n):
             nc.sync.dma_start(out[P * n : P * (n + 1), :], pages[n][:])
 
-        w1q0 = [round_w1(0, 0), round_w1(1, 0)]
+        w1q = [[round_w1(a, b) for a in range(2)] for b in range(2)]
+        for b in range(2):
+            make_h1(b, w1q[b])
         v2_w = gather(tab2_w[:].bitcast(U32), idx2, U32, "v2_w")
         v2_plane = gather(tab2_plane[:], idx2, U8, "v2_plane")
-        make_h1(0, w1q0)
-        w1q1 = [round_w1(0, 1), round_w1(1, 1)]
-        make_h1(1, w1q1)
         zf = [new_z() for c in range(2)]
         w4q = [(w4_w[a], w4_plane[4 * a : P, :]) for a in range(2)]
-        for b in range(2):
-            planes = fleet_planes(b)
-            if b == 0:
-                for c in range(2):
-                    weave(nc.scalar.copy, zf[c], b, planes[:, :, CH * c : CH * (c + 1)])
+        fleet_planes(0)
+        for c in range(2):
+            weave(zf[c], 0, planes[0][:, :, CH * c : CH * (c + 1)])
+        fleet_planes(1)
         w3q = [round_w3(b) for b in range(2)]
-        weave(nc.scalar.copy, zf[0], 1, planes[:, :, 0:CH])
+        for b in range(2):
+            base_sb[b, 1] = load_rows(base, PASS * b, PASS, "late%d" % b)
+        weave(zf[0], 1, planes[1][:, :, 0:CH])
         chunks = [(w4q, quantise_z(zf[0]), idx4, wg2_sb, 0)]
         place_pair(banks[7], *chunks[0], 0)
-        weave(nc.scalar.copy, zf[1], 1, planes[:, :, CH : 2 * CH])
+        weave(zf[1], 1, planes[1][:, :, CH : 2 * CH])
         chunks.append((w4q, quantise_z(zf[1]), idx4, wg2_sb, 1))
         place_pair(banks[4], *chunks[0], 1)
         for c in range(4):

@@ -21,8 +21,8 @@ PASS = P * PACK
 CH = 256
 FLOPS = 2 * (K * H * S + K2 * H * PF + H * N * S + H * N * PF)
 
-H2_BANKS = ((3, 4, 0, 1), (2, 3, 4, 7))
-AHEAD = 4
+H1_BANKS = ((0, 1, 2, 3), (4, 5, 6))
+BACK = ((2, 3), (5, 6))
 H1_ON = {(0, 0): "rows01", (0, 1): "rows00", (1, 0): "rows10", (1, 1): "rows11"}
 
 
@@ -92,16 +92,16 @@ def tile_list_hull_fleet_page_kernel(
         nc.sync.dma_start(w2_in[:].bitcast(I32), w2_words[0].bitcast(I32))
         w1_raw = {(a, 0): load_rows(w1, PASS * a, 0, "rows%d0" % a) for a in range(2)}
         load_plane(w2_plane_in, w2_scales)
-        for a in range(2):
-            w1_raw[a, 1] = load_rows(w1, PASS * a, PASS, "rows%d1" % a)
-        oldest = load_list(pos1, "oldest")
+        w1_raw[0, 1] = load_rows(w1, 0, PASS, "rows01")
         idx2 = load_list(offs2, "idx2")
-        tab2_w = load_words(tab2_words[0], "tab2_w")
         load_plane(tab2_plane, tab2_scales)
+        w1_raw[1, 1] = load_rows(w1, PASS, PASS, "rows11")
+        oldest = load_list(pos1, "oldest")
+        tab2_w = load_words(tab2_words[0], "tab2_w")
         g2 = load_gain(gain2, "g2")
         g1 = load_gain(gain1, "g1")
-        base_sb = {(0, 0): load_rows(base, 0, 0, "base0")}
-        base_sb[1, 0] = load_rows(base, PASS, 0, "base1")
+        base_sb = {(0, jh): load_rows(base, 0, PASS * jh, "base0%d" % jh) for jh in range(2)}
+        base_sb[1, 0] = load_rows(base, PASS, 0, "base10")
         w3_raw = [load_rows(w3, PASS * b, 0, "late%d" % b) for b in range(2)]
         w4_w = [load_words(w4_words[a], "w4_w%d" % a) for a in range(2)]
         load_plane(w4_plane, w4_scales)
@@ -128,13 +128,19 @@ def tile_list_hull_fleet_page_kernel(
             return codes, plane
 
         def round_w1(a, b):
-            wb = stage[a][:].bitcast(BF16)
+            if (a, b) == (1, 1):
+                wb = keep.tile([P, PACK * PASS], BF16, name="wb11", tag="v2_w", align_bytes=64)[:]
+            else:
+                wb = stage[a][:].bitcast(BF16)
             dst = wb.rearrange("p (t m i) -> p m t i", t=PACK, i=PACK)
             src = w1_raw[a, b][:].rearrange("p i (m t) -> p m t i", t=PACK)
             if a == 0:
                 nc.scalar.copy(dst, src)
             else:
-                nc.vector.tensor_copy(dst, src)
+                nc.vector.tensor_copy(
+                    wb.rearrange("p (u e m i) -> p u m e i", u=2, e=2, i=PACK),
+                    w1_raw[a, b][:].rearrange("p i (m u e) -> p u m e i", u=2, e=2),
+                )
             return quantise(wb, keep, "w1q%d%d" % (a, b), 1)
 
         def round_w3(b):
@@ -161,17 +167,19 @@ def tile_list_hull_fleet_page_kernel(
         )
 
         h1 = {}
+        h1_pair = {}
 
         def make_h1(b, w1q):
             for t in range(PACK):
                 if t % 2 == 0:
                     pair = keep.tile([P, 2, S], F32, name="h1_%d%d" % (b, t), tag=H1_ON[b, t // 2])
+                    h1_pair[b, t // 2] = pair
                 rows = pair[:, t % 2, :]
                 h1[b, t] = rows
                 mcols = slice(P * t, P * (t + 1))
                 for jh in range(2):
                     jcols = slice(PASS * jh, PASS * (jh + 1))
-                    bank = banks[(2 * t + jh) % 3]
+                    bank = banks[H1_BANKS[b][(2 * t + jh) % len(H1_BANKS[b])]]
                     for a in range(2):
                         codes, plane = w1q[a]
                         nc.tensor.matmul_mx(
@@ -198,7 +206,7 @@ def tile_list_hull_fleet_page_kernel(
             for t in range(PACK):
                 picked = stage[t // 2][:, PF * (t % 2) : PF * (t % 2 + 1)]
                 nc.vector.tensor_copy(picked, h1[b, t].indirect(oldest[:]))
-                bank = banks[H2_BANKS[b][t]]
+                bank = banks[4 * b + t]
                 col = PASS * b + P * t
                 nc.tensor.matmul_mx(
                     out=bank[:],
@@ -212,11 +220,13 @@ def tile_list_hull_fleet_page_kernel(
                 least = work.tile([P, PF], F32, name="least", tag="least", bufs=4)
                 nc.vector.tensor_tensor(least[:], bank[:], picked, ALU.min)
                 nc.scalar.activation(planes[b][:, t, :], least[:], ACT.Copy, scale=g2[:, b, t : t + 1])
-                if len(tanhs) < AHEAD and True:
-                    vessel_ahead()
+                if b == 0 and t == 0:
+                    added_tanh(0)
+                if b == 0 and t >= 2:
+                    tanhs.append(vessel_tanh(1, P * (t - 2)))
 
         def vessel_tanh(b, j0):
-            bank = banks[5 + (j0 // P) % 2][:].rearrange("p (t j) -> p t j", t=PACK)
+            bank = banks[(j0 // P) % 2][:].rearrange("p (t j) -> p t j", t=PACK)
             given = base_sb[b, j0 // PASS]
             jj = j0 % PASS
             for t in range(PACK):
@@ -224,36 +234,51 @@ def tile_list_hull_fleet_page_kernel(
                                  start=True, stop=False, is_transpose=True)
                 nc.tensor.matmul(bank[:, t, :], lhsT=given[:, t, jj : jj + P], rhs=ident[:],
                                  start=False, stop=True, is_transpose=True)
-            th = work.tile([P, PACK, P], F32, name="th", tag="th", bufs=AHEAD + 2)
+            th = work.tile([P, PACK, P], F32, name="th", tag="th", bufs=4)
             nc.scalar.activation(th[:], bank, ACT.Tanh)
             return th
 
         tanhs = []
 
-        def vessel_ahead():
-            k = len(tanhs)
-            if k < 16:
-                tanhs.append(vessel_tanh(k // 2 % 2, CH * (k // 4) + P * (k % 2)))
+        def sums(c):
+            return base_sb[0, c // 2][:, :, CH * (c % 2) : CH * (c % 2 + 1)]
 
-        def vessel_half(zb, c, b):
-            ths = tanhs[4 * c + 2 * b : 4 * c + 2 * b + 2]
-            rounded = planes[b][:, :, CH * (c % 2) : CH * (c % 2 + 1)]
+        def add_base(jh, u):
+            given = base_sb[0, jh][:, 2 * u : 2 * u + 2, :]
+            nc.gpsimd.tensor_tensor(given, h1_pair[0, u][:, :, PASS * jh : PASS * (jh + 1)], given, ALU.add)
+
+        def added_tanh(c):
+            nc.scalar.activation(sums(c), sums(c), ACT.Tanh)
+
+        def added_half(zb, c):
+            rounded = planes[0][:, :, CH * (c % 2) : CH * (c % 2 + 1)]
+            for t in range(PACK):
+                nc.scalar.activation(rounded[:, t, :], sums(c)[:, t, :], ACT.Copy, scale=g1[:, 0, t : t + 1])
+            if c < 3:
+                added_tanh(c + 1)
+            weave(zb, 0, rounded)
+
+        def turned_half(zb, c):
+            ths = tanhs[2 * c : 2 * c + 2]
+            rounded = planes[1][:, :, CH * (c % 2) : CH * (c % 2 + 1)]
             for u in range(2):
-                bank = banks[2 * b + u][:].rearrange("p (e j) -> p e j", e=2)
+                bank = banks[BACK[c % 2][u]][:].rearrange("p (e j) -> p e j", e=2)
                 for e in range(2):
                     for s in range(2):
                         nc.tensor.transpose(bank[:, e, P * s : P * (s + 1)], ths[s][:, 2 * u + e, :], ident[:])
                 for e in range(2):
                     t = 2 * u + e
-                    nc.scalar.activation(rounded[:, t, :], bank[:, e, :], ACT.Copy, scale=g1[:, b, t : t + 1])
-            vessel_ahead()
-            weave(zb, b, rounded)
-            vessel_ahead()
+                    nc.scalar.activation(rounded[:, t, :], bank[:, e, :], ACT.Copy, scale=g1[:, 1, t : t + 1])
+            if c < 3:
+                tanhs.append(vessel_tanh(1, CH * (c + 1)))
+            weave(zb, 1, rounded)
+            if c < 3:
+                tanhs.append(vessel_tanh(1, CH * (c + 1) + P))
 
         def quantise_z(zb):
             return quantise(zb[:].rearrange("p b j t -> p (b j t)"), work, "zq", 3)
 
-        def product(bank, weights, parts):
+        def product(bank, weights, parts, y=None):
             for e, (n, (codes, plane)) in enumerate(parts):
                 ncols = slice(P * n, P * (n + 1))
                 for b in range(2):
@@ -267,8 +292,9 @@ def tile_list_hull_fleet_page_kernel(
                         start=(b == 0),
                         stop=(b == 1),
                     )
-            y = work.tile([P, 2 * CH], F32, name="y", tag="y", bufs=4)
-            nc.scalar.copy(y[:, 0 : CH * len(parts)], bank[:, 0 : CH * len(parts)])
+            if y is None:
+                y = work.tile([P, 2, CH], F32, name="y", tag="y", bufs=4)[:, 0 : len(parts), :]
+            nc.scalar.copy(y, bank[:, 0 : CH * len(parts)].rearrange("p (e j) -> p e j", j=CH))
             return y
 
         def scatter(n, values, offsets, factors, j0, count):
@@ -279,19 +305,23 @@ def tile_list_hull_fleet_page_kernel(
                 ALU.mult,
             )
 
-        def place_pair(bank, weights, zq, offsets, factors, c, u):
-            y = product(bank, weights, [(2 * u, zq), (2 * u + 1, zq)])
+        def place_pair(bank, weights, zq, offsets, factors, c, u, y=None):
+            y = product(bank, weights, [(2 * u, zq), (2 * u + 1, zq)], y)
             for e in range(2):
-                scatter(2 * u + e, y[:, CH * e : CH * (e + 1)], offsets, factors, CH * c, CH)
+                scatter(2 * u + e, y[:, e, :], offsets, factors, CH * c, CH)
 
         def store(n):
             nc.sync.dma_start(out[P * n : P * (n + 1), :], pages[n][:])
 
-        w1q = [[round_w1(a, b) for a in range(2)] for b in range(2)]
+        w1q = [[round_w1(a, 0) for a in range(2)]]
+        v2_plane = gather(tab2_plane[:], idx2, U8, "v2_plane")
+        w1q.append([round_w1(a, 1) for a in range(2)])
         for b in range(2):
             make_h1(b, w1q[b])
+        for jh in range(2):
+            for u in range(2):
+                add_base(jh, u)
         v2_w = gather(tab2_w[:].bitcast(U32), idx2, U32, "v2_w")
-        v2_plane = gather(tab2_plane[:], idx2, U8, "v2_plane")
         zf = [new_z() for c in range(2)]
         w4q = [(w4_w[a], w4_plane[4 * a : P, :]) for a in range(2)]
         fleet_planes(0)
@@ -299,8 +329,7 @@ def tile_list_hull_fleet_page_kernel(
             weave(zf[c], 0, planes[0][:, :, CH * c : CH * (c + 1)])
         fleet_planes(1)
         w3q = [round_w3(b) for b in range(2)]
-        for b in range(2):
-            base_sb[b, 1] = load_rows(base, PASS * b, PASS, "late%d" % b)
+        base_sb[1, 1] = load_rows(base, PASS, PASS, "late0")
         weave(zf[0], 1, planes[1][:, :, 0:CH])
         chunks = [(w4q, quantise_z(zf[0]), idx4, wg2_sb, 0)]
         place_pair(banks[7], *chunks[0], 0)
@@ -309,22 +338,22 @@ def tile_list_hull_fleet_page_kernel(
         place_pair(banks[4], *chunks[0], 1)
         for c in range(4):
             zb = new_z()
-            vessel_half(zb, c, 0)
-            place_pair(banks[1], *chunks[-1], 0)
-            vessel_half(zb, c, 1)
+            added_half(zb, c)
+            place_pair(banks[7], *chunks[-1], 0, sums(c)[:, 2:4, :])
+            turned_half(zb, c)
             zq = quantise_z(zb)
             if c < 3:
-                place_pair(banks[3], *chunks[-1], 1)
+                place_pair(banks[BACK[c % 2][1]], *chunks[-1], 1)
             chunks.append((w3q, zq, idx3, wg1_sb, c))
         before, last = chunks[-2][1], chunks[-1][1]
-        y = product(banks[3], w3q, [(2, before)])
-        scatter(2, y[:, 0:CH], idx3, wg1_sb, 2 * CH, CH)
+        y = product(banks[6], w3q, [(2, before)])
+        scatter(2, y[:, 0, :], idx3, wg1_sb, 2 * CH, CH)
         place_pair(banks[7], *chunks[-1], 0)
         store(0)
         store(1)
         y = product(banks[4], w3q, [(2, last)])
-        scatter(2, y[:, 0:CH], idx3, wg1_sb, 3 * CH, CH)
+        scatter(2, y[:, 0, :], idx3, wg1_sb, 3 * CH, CH)
         store(2)
-        y = product(banks[5], w3q, [(3, before), (3, last)])
-        scatter(3, y[:], idx3, wg1_sb, 2 * CH, 2 * CH)
+        y = product(banks[0], w3q, [(3, before), (3, last)])
+        scatter(3, y.rearrange("p e j -> p (e j)"), idx3, wg1_sb, 2 * CH, 2 * CH)
         store(3)

@@ -14,16 +14,24 @@ FP4X4 = mybir.dt.float4_e2m1fn_x4
 ALU = mybir.AluOpType
 ACT = mybir.ActivationFunctionType
 
-K, K2, H, N, T, S, PF, T2 = 1024, 512, 1024, 512, 2048, 1024, 512, 2048
+K, K2, H, N, T, S, FLEETS = 1024, 512, 1024, 512, 2048, 1024, 512
+FLOPS = 2 * (K * H * S + K2 * H * FLEETS + H * N * S + H * N * FLEETS)
+
 P = 128
 PACK = 4
 PASS = P * PACK
-CH = 256
-FLOPS = 2 * (K * H * S + K2 * H * PF + H * N * S + H * N * PF)
+CHUNK = 256
+CHUNKS = S // CHUNK
+GROUP = 16
+
+FIRST_ADDED = 1
 
 H1_BANKS = ((0, 1, 2, 3), (4, 5, 6))
-BACK = ((2, 3), (5, 6))
-H1_ON = {(0, 0): "rows01", (0, 1): "rows00", (1, 0): "rows10", (1, 1): "rows11"}
+SUM_BANKS = (0, 1)
+TURN_BANKS = ((2, 3), (5, 6))
+SPARE_BANKS = (7, 4)
+
+H1_BUFFER = {(0, 0): (0, 1), (0, 1): (0, 0), (1, 0): (1, 0), (1, 1): (1, 1)}
 
 
 def tile_list_hull_fleet_page_kernel(
@@ -38,6 +46,7 @@ def tile_list_hull_fleet_page_kernel(
         psum = ctx.enter_context(tc.psum_pool(name="psum", bufs=1))
         banks = [psum.tile([P, PASS], F32, name="bank%d" % i) for i in range(8)]
 
+
         def load_list(src, name):
             tile = lists.tile([P, src.shape[1]], U16, name=name)
             nc.sync.dma_start(tile[:], src)
@@ -50,10 +59,10 @@ def tile_list_hull_fleet_page_kernel(
 
         def load_plane(plane, scales):
             rows = 4 * scales.shape[0]
-            for q in range(4):
+            for quadrant in range(4):
                 nc.sync.dma_start(
-                    plane[32 * q : 32 * q + rows, :].bitcast(I32),
-                    scales[:, 4 * q : 4 * q + 4, :].bitcast(I32),
+                    plane[32 * quadrant : 32 * quadrant + rows, :].bitcast(I32),
+                    scales[:, 4 * quadrant : 4 * quadrant + 4, :].bitcast(I32),
                 )
 
         def load_words(words, name):
@@ -61,10 +70,10 @@ def tile_list_hull_fleet_page_kernel(
             nc.sync.dma_start(tile[:], words.rearrange("p c i -> p (c i)").bitcast(I32))
             return tile
 
-        def load_rows(src, row0, col0, name):
+        def load_block(src, row_half, col_half, name):
             tile = keep.tile([P, PACK, PASS], F32, name=name)
-            rows = src[row0 : row0 + PASS, col0 : col0 + PASS]
-            nc.sync.dma_start(tile[:], rows.rearrange("(p i) c -> p i c", i=PACK))
+            block = src[PASS * row_half : PASS * (row_half + 1), PASS * col_half : PASS * (col_half + 1)]
+            nc.sync.dma_start(tile[:], block.rearrange("(p i) c -> p i c", i=PACK))
             return tile
 
         def load_gain(src, name):
@@ -88,35 +97,35 @@ def tile_list_hull_fleet_page_kernel(
         tab_w = [load_words(tab_words[0], "tab_w0")]
         load_plane(tab_plane, tab_scales)
         tab_w.append(load_words(tab_words[1], "tab_w1"))
+        w1_rows = {(a, 0): load_block(w1, a, 0, "w1_rows%d0" % a) for a in range(2)}
+        load_plane(w2_plane_in, w2_scales)
+        w1_rows[0, 1] = load_block(w1, 0, 1, "w1_rows01")
         w2_in = keep.tile([P, 2 * H], U8, name="w2_in", align_bytes=64)
         nc.sync.dma_start(w2_in[:].bitcast(I32), w2_words[0].bitcast(I32))
-        w1_raw = {(a, 0): load_rows(w1, PASS * a, 0, "rows%d0" % a) for a in range(2)}
-        load_plane(w2_plane_in, w2_scales)
-        w1_raw[0, 1] = load_rows(w1, 0, PASS, "rows01")
         idx2 = load_list(offs2, "idx2")
         load_plane(tab2_plane, tab2_scales)
-        w1_raw[1, 1] = load_rows(w1, PASS, PASS, "rows11")
+        w1_rows[1, 1] = load_block(w1, 1, 1, "w1_rows11")
         oldest = load_list(pos1, "oldest")
         tab2_w = load_words(tab2_words[0], "tab2_w")
         g2 = load_gain(gain2, "g2")
         g1 = load_gain(gain1, "g1")
-        base_sb = {(0, jh): load_rows(base, 0, PASS * jh, "base0%d" % jh) for jh in range(2)}
-        base_sb[1, 0] = load_rows(base, PASS, 0, "base10")
-        w3_raw = [load_rows(w3, PASS * b, 0, "late%d" % b) for b in range(2)]
-        w4_w = [load_words(w4_words[a], "w4_w%d" % a) for a in range(2)]
+        base_rows = {(b, 0): load_block(base, b, 0, "base_rows%d0" % b) for b in range(2)}
+        w3_rows = [load_block(w3, b, 0, "w3_rows%d" % b) for b in range(2)]
+        base_rows[0, 1] = load_block(base, 0, 1, "base_rows01")
+        w4_w = [load_words(w4_words[b], "w4_w%d" % b) for b in range(2)]
         load_plane(w4_plane, w4_scales)
         idx4 = load_list(offs4, "idx4")
         wg2_sb = load_plain(wg2, "wg2_sb")
-        pages = [load_plain(page1[n * P : (n + 1) * P, :], "page%d" % n) for n in range(4)]
+        pages = [load_plain(page1[n * P : (n + 1) * P, :], "page%d" % n) for n in range(N // P)]
         idx3 = load_list(offs3, "idx3")
         wg1_sb = load_plain(wg1, "wg1_sb")
 
-        stage = [keep.tile([P, 2 * PF], F32, name="stage%d" % i, align_bytes=64) for i in range(2)]
-        planes = [keep.tile([P, PACK, PF], BF16, name="planes%d" % b) for b in range(2)]
+        stage = [keep.tile([P, 2 * FLEETS], F32, name="stage%d" % i, align_bytes=64) for i in range(2)]
+        slices = [keep.tile([P, PACK, FLEETS], BF16, name="slices%d" % b) for b in range(2)]
+
 
         def gather(window, offsets, dtype, name):
-            count = 16 * offsets.shape[1]
-            picked = keep.tile([P, count], dtype, name=name, align_bytes=64)
+            picked = keep.tile([P, GROUP * offsets.shape[1]], dtype, name=name, align_bytes=64)
             nc.vector.tensor_copy(picked[:], window.indirect(offsets[:]))
             return picked
 
@@ -127,29 +136,30 @@ def tile_list_hull_fleet_page_kernel(
             nc.vector.quantize_mx(out=codes[:].bitcast(FP8X4), scales=plane[:], in_=src)
             return codes, plane
 
-        def round_w1(a, b):
+        def quantise_w1(a, b):
             if (a, b) == (1, 1):
-                wb = keep.tile([P, PACK * PASS], BF16, name="wb11", tag="v2_w", align_bytes=64)[:]
+                rounded = keep.tile([P, PACK * PASS], BF16, name="w1_last", tag="v2_w", align_bytes=64)[:]
             else:
-                wb = stage[a][:].bitcast(BF16)
-            dst = wb.rearrange("p (t m i) -> p m t i", t=PACK, i=PACK)
-            src = w1_raw[a, b][:].rearrange("p i (m t) -> p m t i", t=PACK)
+                rounded = stage[a][:].bitcast(BF16)
             if a == 0:
-                nc.scalar.copy(dst, src)
+                nc.scalar.copy(
+                    rounded.rearrange("p (t m i) -> p m t i", t=PACK, i=PACK),
+                    w1_rows[a, b][:].rearrange("p i (m t) -> p m t i", t=PACK),
+                )
             else:
                 nc.vector.tensor_copy(
-                    wb.rearrange("p (u e m i) -> p u m e i", u=2, e=2, i=PACK),
-                    w1_raw[a, b][:].rearrange("p i (m u e) -> p u m e i", u=2, e=2),
+                    rounded.rearrange("p (u e m i) -> p u m e i", u=2, e=2, i=PACK),
+                    w1_rows[a, b][:].rearrange("p i (m u e) -> p u m e i", u=2, e=2),
                 )
-            return quantise(wb, keep, "w1q%d%d" % (a, b), 1)
+            return quantise(rounded, keep, "w1q%d%d" % (a, b), 1)
 
-        def round_w3(b):
-            wb = stage[b][:].bitcast(BF16)
+        def quantise_w3(b):
+            rounded = stage[b][:].bitcast(BF16)
             nc.vector.tensor_copy(
-                wb.rearrange("p (c e i) -> p c i e", e=4, i=PACK),
-                w3_raw[b][:].rearrange("p i (c e) -> p c i e", e=4),
+                rounded.rearrange("p (c e i) -> p c i e", e=4, i=PACK),
+                w3_rows[b][:].rearrange("p i (c e) -> p c i e", e=4),
             )
-            return quantise(wb, keep, "w3q%d" % b, 1)
+            return quantise(rounded, keep, "w3q%d" % b, 1)
 
         v_w = [gather(tab_w[0][:].bitcast(U32), idx, U32, "v_w0")]
         v_plane = gather(tab_plane[:], idx, U8, "v_plane")
@@ -166,47 +176,91 @@ def tile_list_hull_fleet_page_kernel(
             w2_plane_in[:].rearrange("p (b m t) -> p b t m", b=2, t=PACK),
         )
 
-        h1 = {}
-        h1_pair = {}
+        w1q = [[quantise_w1(a, 0) for a in range(2)]]
+        v2_plane = gather(tab2_plane[:], idx2, U8, "v2_plane")
+        w1q.append([quantise_w1(a, 1) for a in range(2)])
 
-        def make_h1(b, w1q):
+
+        h1_pairs = {}
+
+        def h1_slice(b, t):
+            return h1_pairs[b, t // 2][:, t % 2, :]
+
+        for b in range(2):
             for t in range(PACK):
                 if t % 2 == 0:
-                    pair = keep.tile([P, 2, S], F32, name="h1_%d%d" % (b, t), tag=H1_ON[b, t // 2])
-                    h1_pair[b, t // 2] = pair
-                rows = pair[:, t % 2, :]
-                h1[b, t] = rows
-                mcols = slice(P * t, P * (t + 1))
+                    h1_pairs[b, t // 2] = keep.tile(
+                        [P, 2, S], F32, name="h1_%d%d" % (b, t), tag="w1_rows%d%d" % H1_BUFFER[b, t // 2]
+                    )
+                rcols = slice(P * t, P * (t + 1))
                 for jh in range(2):
                     jcols = slice(PASS * jh, PASS * (jh + 1))
                     bank = banks[H1_BANKS[b][(2 * t + jh) % len(H1_BANKS[b])]]
                     for a in range(2):
-                        codes, plane = w1q[a]
+                        codes, plane = w1q[b][a]
                         nc.tensor.matmul_mx(
                             out=bank[:],
-                            lhsT=codes[:, mcols].bitcast(FP8X4),
-                            lhsT_scale=plane[:, mcols],
+                            lhsT=codes[:, rcols].bitcast(FP8X4),
+                            lhsT_scale=plane[:, rcols],
                             rhs=v_w[a][:, jcols].bitcast(FP8X4),
                             rhs_scale=v_plane[4 * a : P, jcols],
                             start=(a == 0),
                             stop=(a == 1),
                         )
-                    nc.scalar.copy(rows[:, jcols], bank[:])
+                    nc.scalar.copy(h1_slice(b, t)[:, jcols], bank[:])
+
+        v2_w = gather(tab2_w[:].bitcast(U32), idx2, U32, "v2_w")
+
 
         def new_z():
-            return work.tile([P, 2, CH, PACK], BF16, name="zb", tag="zb", align_bytes=64)
+            return work.tile([P, 2, CHUNK, PACK], BF16, name="z", align_bytes=64)
 
-        def weave(zb, b, rows):
+        def interleave(z, b, rows):
             nc.scalar.copy(
-                zb[:, b].rearrange("p (c e) t -> p c t e", e=4),
+                z[:, b].rearrange("p (c e) t -> p c t e", e=4),
                 rows.rearrange("p t (c e) -> p c t e", e=4),
             )
 
-        def fleet_planes(b):
+        def quantise_z(z):
+            return quantise(z[:].rearrange("p b j t -> p (b j t)"), work, "zq", 3)
+
+        def is_added(c, b):
+            return b == 0 and c >= FIRST_ADDED
+
+        def added(c):
+            return sum_buffers[c].rearrange("p (t j) -> p t j", t=PACK)
+
+        transposed_tanh = {}
+
+        def tanh_ahead(c, b, s):
+            given = base_rows[b, c // 2]
+            j0, jj = CHUNK * c, CHUNK * (c % 2)
+            if not is_added(c, b):
+                bank = banks[SUM_BANKS[s]][:].rearrange("p (t j) -> p t j", t=PACK)
+                for t in range(PACK):
+                    terms = (h1_slice(b, t)[:, j0 + P * s : j0 + P * (s + 1)], given[:, t, jj + P * s : jj + P * (s + 1)])
+                    for e, term in enumerate(terms):
+                        nc.tensor.matmul(
+                            bank[:, t, :], lhsT=term, rhs=ident[:], start=(e == 0), stop=(e == 1), is_transpose=True
+                        )
+                tanh = work.tile([P, PACK, P], F32, name="tanh", bufs=6)
+                nc.scalar.activation(tanh[:], bank, ACT.Tanh)
+                transposed_tanh[c, b, s] = tanh
+            elif s == 0:
+                for u in range(2):
+                    nc.vector.tensor_tensor(
+                        added(c)[:, 2 * u : 2 * u + 2, :],
+                        h1_pairs[b, u][:, :, j0 : j0 + CHUNK],
+                        given[:, 2 * u : 2 * u + 2, jj : jj + CHUNK],
+                        ALU.add,
+                    )
+                nc.scalar.activation(added(c), added(c), ACT.Tanh)
+
+        def fleet_slices(b):
             for t in range(PACK):
-                picked = stage[t // 2][:, PF * (t % 2) : PF * (t % 2 + 1)]
-                nc.vector.tensor_copy(picked, h1[b, t].indirect(oldest[:]))
-                bank = banks[4 * b + t]
+                picked = stage[t // 2][:, FLEETS * (t % 2) : FLEETS * (t % 2 + 1)]
+                nc.vector.tensor_copy(picked, h1_slice(b, t).indirect(oldest[:]))
+                bank = banks[PACK * b + t]
                 col = PASS * b + P * t
                 nc.tensor.matmul_mx(
                     out=bank[:],
@@ -217,143 +271,117 @@ def tile_list_hull_fleet_page_kernel(
                     start=True,
                     stop=True,
                 )
-                least = work.tile([P, PF], F32, name="least", tag="least", bufs=4)
+                least = work.tile([P, FLEETS], F32, name="least", bufs=PACK)
                 nc.vector.tensor_tensor(least[:], bank[:], picked, ALU.min)
-                nc.scalar.activation(planes[b][:, t, :], least[:], ACT.Copy, scale=g2[:, b, t : t + 1])
-                if b == 0 and t == 0:
-                    added_tanh(0)
-                if b == 0 and t >= 2:
-                    tanhs.append(vessel_tanh(1, P * (t - 2)))
+                nc.scalar.activation(slices[b][:, t, :], least[:], ACT.Copy, scale=g2[:, b, t : t + 1])
+                if b == 0:
+                    tanh_ahead(0, t // 2, t % 2)
 
-        def vessel_tanh(b, j0):
-            bank = banks[(j0 // P) % 2][:].rearrange("p (t j) -> p t j", t=PACK)
-            given = base_sb[b, j0 // PASS]
-            jj = j0 % PASS
-            for t in range(PACK):
-                nc.tensor.matmul(bank[:, t, :], lhsT=h1[b, t][:, j0 : j0 + P], rhs=ident[:],
-                                 start=True, stop=False, is_transpose=True)
-                nc.tensor.matmul(bank[:, t, :], lhsT=given[:, t, jj : jj + P], rhs=ident[:],
-                                 start=False, stop=True, is_transpose=True)
-            th = work.tile([P, PACK, P], F32, name="th", tag="th", bufs=4)
-            nc.scalar.activation(th[:], bank, ACT.Tanh)
-            return th
+        turns = []
 
-        tanhs = []
+        def vessel_half(z, c, b):
+            rounded = slices[b][:, :, CHUNK * (c % 2) : CHUNK * (c % 2 + 1)]
+            if is_added(c, b):
+                for t in range(PACK):
+                    nc.scalar.activation(rounded[:, t, :], added(c)[:, t, :], ACT.Copy, scale=g1[:, b, t : t + 1])
+            else:
+                turns.append(TURN_BANKS[len(turns) % 2])
+                for u in range(2):
+                    bank = banks[turns[-1][u]][:].rearrange("p (e j) -> p e j", e=2)
+                    for e in range(2):
+                        for s in range(2):
+                            nc.tensor.transpose(
+                                bank[:, e, P * s : P * (s + 1)], transposed_tanh[c, b, s][:, 2 * u + e, :], ident[:]
+                            )
+                    for e in range(2):
+                        t = 2 * u + e
+                        nc.scalar.activation(rounded[:, t, :], bank[:, e, :], ACT.Copy, scale=g1[:, b, t : t + 1])
+            if c + 1 < CHUNKS:
+                tanh_ahead(c + 1, b, 0)
+            interleave(z, b, rounded)
+            if c + 1 < CHUNKS:
+                tanh_ahead(c + 1, b, 1)
 
-        def sums(c):
-            return base_sb[0, c // 2][:, :, CH * (c % 2) : CH * (c % 2 + 1)]
 
-        def add_base(jh, u):
-            given = base_sb[0, jh][:, 2 * u : 2 * u + 2, :]
-            nc.gpsimd.tensor_tensor(given, h1_pair[0, u][:, :, PASS * jh : PASS * (jh + 1)], given, ALU.add)
+        def new_y(count):
+            return work.tile([P, 2, CHUNK], F32, name="y", bufs=4)[:, 0:count, :]
 
-        def added_tanh(c):
-            nc.scalar.activation(sums(c), sums(c), ACT.Tanh)
-
-        def added_half(zb, c):
-            rounded = planes[0][:, :, CH * (c % 2) : CH * (c % 2 + 1)]
-            for t in range(PACK):
-                nc.scalar.activation(rounded[:, t, :], sums(c)[:, t, :], ACT.Copy, scale=g1[:, 0, t : t + 1])
-            if c < 3:
-                added_tanh(c + 1)
-            weave(zb, 0, rounded)
-
-        def turned_half(zb, c):
-            ths = tanhs[2 * c : 2 * c + 2]
-            rounded = planes[1][:, :, CH * (c % 2) : CH * (c % 2 + 1)]
-            for u in range(2):
-                bank = banks[BACK[c % 2][u]][:].rearrange("p (e j) -> p e j", e=2)
-                for e in range(2):
-                    for s in range(2):
-                        nc.tensor.transpose(bank[:, e, P * s : P * (s + 1)], ths[s][:, 2 * u + e, :], ident[:])
-                for e in range(2):
-                    t = 2 * u + e
-                    nc.scalar.activation(rounded[:, t, :], bank[:, e, :], ACT.Copy, scale=g1[:, 1, t : t + 1])
-            if c < 3:
-                tanhs.append(vessel_tanh(1, CH * (c + 1)))
-            weave(zb, 1, rounded)
-            if c < 3:
-                tanhs.append(vessel_tanh(1, CH * (c + 1) + P))
-
-        def quantise_z(zb):
-            return quantise(zb[:].rearrange("p b j t -> p (b j t)"), work, "zq", 3)
-
-        def product(bank, weights, parts, y=None):
+        def product(bank, weights, parts, y):
             for e, (n, (codes, plane)) in enumerate(parts):
                 ncols = slice(P * n, P * (n + 1))
                 for b in range(2):
                     wcodes, wplane = weights[b]
                     nc.tensor.matmul_mx(
-                        out=bank[:, CH * e : CH * (e + 1)],
+                        out=bank[:, CHUNK * e : CHUNK * (e + 1)],
                         lhsT=wcodes[:, ncols].bitcast(FP8X4),
                         lhsT_scale=wplane[:, ncols],
-                        rhs=codes[:, CH * b : CH * (b + 1)].bitcast(FP8X4),
-                        rhs_scale=plane[:, CH * b : CH * (b + 1)],
+                        rhs=codes[:, CHUNK * b : CHUNK * (b + 1)].bitcast(FP8X4),
+                        rhs_scale=plane[:, CHUNK * b : CHUNK * (b + 1)],
                         start=(b == 0),
                         stop=(b == 1),
                     )
-            if y is None:
-                y = work.tile([P, 2, CH], F32, name="y", tag="y", bufs=4)[:, 0 : len(parts), :]
-            nc.scalar.copy(y, bank[:, 0 : CH * len(parts)].rearrange("p (e j) -> p e j", j=CH))
-            return y
+            nc.scalar.copy(y, bank[:, 0 : CHUNK * len(parts)].rearrange("p (e j) -> p e j", j=CHUNK))
 
         def scatter(n, values, offsets, factors, j0, count):
             nc.vector.tensor_tensor(
-                pages[n][:].indirect(offsets[:, j0 // 16 : (j0 + count) // 16]),
+                pages[n][:].indirect(offsets[:, j0 // GROUP : (j0 + count) // GROUP]),
                 values,
                 factors[:, j0 : j0 + count],
                 ALU.mult,
             )
 
-        def place_pair(bank, weights, zq, offsets, factors, c, u, y=None):
-            y = product(bank, weights, [(2 * u, zq), (2 * u + 1, zq)], y)
+        def place_pair(bank, chunk, u, y):
+            weights, zq, offsets, factors, c = chunk
+            product(banks[bank], weights, [(2 * u, zq), (2 * u + 1, zq)], y)
             for e in range(2):
-                scatter(2 * u + e, y[:, e, :], offsets, factors, CH * c, CH)
+                scatter(2 * u + e, y[:, e, :], offsets, factors, CHUNK * c, CHUNK)
 
         def store(n):
             nc.sync.dma_start(out[P * n : P * (n + 1), :], pages[n][:])
 
-        w1q = [[round_w1(a, 0) for a in range(2)]]
-        v2_plane = gather(tab2_plane[:], idx2, U8, "v2_plane")
-        w1q.append([round_w1(a, 1) for a in range(2)])
-        for b in range(2):
-            make_h1(b, w1q[b])
-        for jh in range(2):
-            for u in range(2):
-                add_base(jh, u)
-        v2_w = gather(tab2_w[:].bitcast(U32), idx2, U32, "v2_w")
-        zf = [new_z() for c in range(2)]
-        w4q = [(w4_w[a], w4_plane[4 * a : P, :]) for a in range(2)]
-        fleet_planes(0)
+        z_fleets = [new_z() for c in range(2)]
+        w4q = [(w4_w[b], w4_plane[4 * b : P, :]) for b in range(2)]
+        fleet_slices(0)
         for c in range(2):
-            weave(zf[c], 0, planes[0][:, :, CH * c : CH * (c + 1)])
-        fleet_planes(1)
-        w3q = [round_w3(b) for b in range(2)]
-        base_sb[1, 1] = load_rows(base, PASS, PASS, "late0")
-        weave(zf[0], 1, planes[1][:, :, 0:CH])
-        chunks = [(w4q, quantise_z(zf[0]), idx4, wg2_sb, 0)]
-        place_pair(banks[7], *chunks[0], 0)
-        weave(zf[1], 1, planes[1][:, :, CH : 2 * CH])
-        chunks.append((w4q, quantise_z(zf[1]), idx4, wg2_sb, 1))
-        place_pair(banks[4], *chunks[0], 1)
-        for c in range(4):
-            zb = new_z()
-            added_half(zb, c)
-            place_pair(banks[7], *chunks[-1], 0, sums(c)[:, 2:4, :])
-            turned_half(zb, c)
-            zq = quantise_z(zb)
-            if c < 3:
-                place_pair(banks[BACK[c % 2][1]], *chunks[-1], 1)
-            chunks.append((w3q, zq, idx3, wg1_sb, c))
-        before, last = chunks[-2][1], chunks[-1][1]
-        y = product(banks[6], w3q, [(2, before)])
-        scatter(2, y[:, 0, :], idx3, wg1_sb, 2 * CH, CH)
-        place_pair(banks[7], *chunks[-1], 0)
+            interleave(z_fleets[c], 0, slices[0][:, :, CHUNK * c : CHUNK * (c + 1)])
+        fleet_slices(1)
+        w3q = [quantise_w3(b) for b in range(2)]
+        base_rows[1, 1] = load_block(base, 1, 1, "w3_rows0")
+        last_sum = keep.tile([P, PACK * CHUNK], F32, name="last_sum", tag="w3_rows1")
+        sum_buffers = {1: stage[1][:], 2: stage[0][:], 3: last_sum[:]}
+        interleave(z_fleets[0], 1, slices[1][:, :, 0:CHUNK])
+        first = (w4q, quantise_z(z_fleets[0]), idx4, wg2_sb, 0)
+        place_pair(SPARE_BANKS[0], first, 0, new_y(2))
+        interleave(z_fleets[1], 1, slices[1][:, :, CHUNK : 2 * CHUNK])
+        behind = (w4q, quantise_z(z_fleets[1]), idx4, wg2_sb, 1)
+        place_pair(SPARE_BANKS[1], first, 1, new_y(2))
+
+        for c in range(CHUNKS):
+            z = new_z()
+            vessel_half(z, c, 0)
+            if is_added(c, 0):
+                place_pair(SPARE_BANKS[0], behind, 0, added(c)[:, 2:4, :])
+            else:
+                place_pair(turns[-1][1], behind, 0, new_y(2))
+            vessel_half(z, c, 1)
+            zq = quantise_z(z)
+            if c + 1 < CHUNKS:
+                place_pair(turns[-1][1], behind, 1, new_y(2))
+                behind = (w3q, zq, idx3, wg1_sb, c)
+
+        last = (w3q, zq, idx3, wg1_sb, CHUNKS - 1)
+        j_behind, j_last = S - 2 * CHUNK, S - CHUNK
+        y = new_y(1)
+        product(banks[turns[-1][1]], w3q, [(2, behind[1])], y)
+        scatter(2, y[:, 0, :], idx3, wg1_sb, j_behind, CHUNK)
+        place_pair(SPARE_BANKS[0], last, 0, new_y(2))
         store(0)
         store(1)
-        y = product(banks[4], w3q, [(2, last)])
-        scatter(2, y[:, 0, :], idx3, wg1_sb, 3 * CH, CH)
+        y = new_y(1)
+        product(banks[SPARE_BANKS[1]], w3q, [(2, zq)], y)
+        scatter(2, y[:, 0, :], idx3, wg1_sb, j_last, CHUNK)
         store(2)
-        y = product(banks[0], w3q, [(3, before), (3, last)])
-        scatter(3, y.rearrange("p e j -> p (e j)"), idx3, wg1_sb, 2 * CH, 2 * CH)
+        y = new_y(2)
+        product(banks[SUM_BANKS[0]], w3q, [(3, behind[1]), (3, zq)], y)
+        scatter(3, y.rearrange("p e j -> p (e j)"), idx3, wg1_sb, j_behind, 2 * CHUNK)
         store(3)

@@ -330,11 +330,15 @@ def tile_list_hull_fleet_page_kernel(
                 ALU.mult,
             )
 
-        def place_pair(bank, chunk, u, y):
-            weights, zq, offsets, factors, c = chunk
-            product(banks[bank], weights, [(2 * u, zq), (2 * u + 1, zq)], y)
+        def place_fleets(bank, n):
+            y = new_y(2)
+            product(banks[bank], w4q, [(n, zq) for zq in zq_fleets], y)
+            scatter(n, y.rearrange("p e j -> p (e j)"), idx4, wg2_sb, 0, FLEETS)
+
+        def place_vessels(bank, c, u, y):
+            product(banks[bank], w3q, [(2 * u, zq_vessels[c]), (2 * u + 1, zq_vessels[c])], y)
             for e in range(2):
-                scatter(2 * u + e, y[:, e, :], offsets, factors, CHUNK * c, CHUNK)
+                scatter(2 * u + e, y[:, e, :], idx3, wg1_sb, CHUNK * c, CHUNK)
 
         def store(n):
             nc.sync.dma_start(out[P * n : P * (n + 1), :], pages[n][:])
@@ -349,39 +353,40 @@ def tile_list_hull_fleet_page_kernel(
         base_rows[1, 1] = load_block(base, 1, 1, "w3_rows0")
         last_sum = keep.tile([P, PACK * CHUNK], F32, name="last_sum", tag="w3_rows1")
         sum_buffers = {1: stage[1][:], 2: stage[0][:], 3: last_sum[:]}
-        interleave(z_fleets[0], 1, slices[1][:, :, 0:CHUNK])
-        first = (w4q, quantise_z(z_fleets[0]), idx4, wg2_sb, 0)
-        place_pair(SPARE_BANKS[0], first, 0, new_y(2))
-        interleave(z_fleets[1], 1, slices[1][:, :, CHUNK : 2 * CHUNK])
-        behind = (w4q, quantise_z(z_fleets[1]), idx4, wg2_sb, 1)
-        place_pair(SPARE_BANKS[1], first, 1, new_y(2))
+        zq_fleets = []
+        for c in range(2):
+            interleave(z_fleets[c], 1, slices[1][:, :, CHUNK * c : CHUNK * (c + 1)])
+            zq_fleets.append(quantise_z(z_fleets[c]))
+        for n in range(2):
+            place_fleets(SPARE_BANKS[n], n)
 
+        zq_vessels = []
         for c in range(CHUNKS):
             z = new_z()
             vessel_half(z, c, 0)
-            if is_added(c, 0):
-                place_pair(SPARE_BANKS[0], behind, 0, added(c)[:, 2:4, :])
+            if c == 0:
+                place_fleets(turns[-1][1], 2)
             else:
-                place_pair(turns[-1][1], behind, 0, new_y(2))
+                place_vessels(SPARE_BANKS[0], c - 1, 0, added(c)[:, 2:4, :])
             vessel_half(z, c, 1)
-            zq = quantise_z(z)
-            if c + 1 < CHUNKS:
-                place_pair(turns[-1][1], behind, 1, new_y(2))
-                behind = (w3q, zq, idx3, wg1_sb, c)
+            zq_vessels.append(quantise_z(z))
+            if c == 0:
+                place_fleets(turns[-1][1], 3)
+            elif c + 1 < CHUNKS:
+                place_vessels(turns[-1][1], c - 1, 1, new_y(2))
 
-        last = (w3q, zq, idx3, wg1_sb, CHUNKS - 1)
-        j_behind, j_last = S - 2 * CHUNK, S - CHUNK
+        before, last = CHUNKS - 2, CHUNKS - 1
         y = new_y(1)
-        product(banks[turns[-1][1]], w3q, [(2, behind[1])], y)
-        scatter(2, y[:, 0, :], idx3, wg1_sb, j_behind, CHUNK)
-        place_pair(SPARE_BANKS[0], last, 0, new_y(2))
+        product(banks[turns[-1][1]], w3q, [(2, zq_vessels[before])], y)
+        scatter(2, y[:, 0, :], idx3, wg1_sb, CHUNK * before, CHUNK)
+        place_vessels(SPARE_BANKS[0], last, 0, new_y(2))
         store(0)
         store(1)
         y = new_y(1)
-        product(banks[SPARE_BANKS[1]], w3q, [(2, zq)], y)
-        scatter(2, y[:, 0, :], idx3, wg1_sb, j_last, CHUNK)
+        product(banks[SPARE_BANKS[1]], w3q, [(2, zq_vessels[last])], y)
+        scatter(2, y[:, 0, :], idx3, wg1_sb, CHUNK * last, CHUNK)
         store(2)
         y = new_y(2)
-        product(banks[SUM_BANKS[0]], w3q, [(3, behind[1]), (3, zq)], y)
-        scatter(3, y.rearrange("p e j -> p (e j)"), idx3, wg1_sb, j_behind, 2 * CHUNK)
+        product(banks[SUM_BANKS[0]], w3q, [(3, zq_vessels[before]), (3, zq_vessels[last])], y)
+        scatter(3, y.rearrange("p e j -> p (e j)"), idx3, wg1_sb, CHUNK * before, 2 * CHUNK)
         store(3)

from contextlib import ExitStack

import concourse.mybir as mybir
from concourse.masks import make_identity

F32 = mybir.dt.float32
BF16 = mybir.dt.bfloat16
I32 = mybir.dt.int32
U32 = mybir.dt.uint32
U16 = mybir.dt.uint16
U8 = mybir.dt.uint8
FP8X4 = mybir.dt.float8_e4m3fn_x4
FP4X4 = mybir.dt.float4_e2m1fn_x4
ALU = mybir.AluOpType
ACT = mybir.ActivationFunctionType

K, K2, H, N, T, S, FLEETS = 1024, 512, 1024, 512, 2048, 1024, 512
FLOPS = 2 * (K * H * S + K2 * H * FLEETS + H * N * S + H * N * FLEETS)

P = 128
PACK = 4
PASS = P * PACK
CHUNK = 256
CHUNKS = S // CHUNK
GROUP = 16

FIRST_ADDED = 1

H1_BANKS = ((0, 1, 2, 3), (4, 5, 6))
SUM_BANKS = (0, 1)
TURN_BANKS = ((2, 3), (5, 6))
SPARE_BANKS = (7, 4)

H1_BUFFER = {(0, 0): (0, 1), (0, 1): (0, 0), (1, 0): (1, 0), (1, 1): (1, 1)}


def tile_list_hull_fleet_page_kernel(
    tc, tab_words, tab_scales, tab2_words, tab2_scales, offs, offs2, pos1, offs3, offs4,
    w1, w2_words, w2_scales, base, gain1, gain2, w3, w4_words, w4_scales, page1, wg1, wg2, out,
):
    nc = tc.nc
    with ExitStack() as ctx:
        lists = ctx.enter_context(tc.tile_pool(name="lists", bufs=1))
        keep = ctx.enter_context(tc.tile_pool(name="keep", bufs=1))
        work = ctx.enter_context(tc.tile_pool(name="work", bufs=2))
        psum = ctx.enter_context(tc.psum_pool(name="psum", bufs=1))
        banks = [psum.tile([P, PASS], F32, name="bank%d" % i) for i in range(8)]


        def load_list(src, name):
            tile = lists.tile([P, src.shape[1]], U16, name=name)
            nc.sync.dma_start(tile[:], src)
            return tile

        def zeroed_plane(width, name):
            plane = keep.tile([P, width], U8, name=name, align_bytes=64)
            nc.vector.memset(plane[:].bitcast(I32), 0)
            return plane

        def load_plane(plane, scales):
            rows = 4 * scales.shape[0]
            for quadrant in range(4):
                nc.sync.dma_start(
                    plane[32 * quadrant : 32 * quadrant + rows, :].bitcast(I32),
                    scales[:, 4 * quadrant : 4 * quadrant + 4, :].bitcast(I32),
                )

        def load_words(words, name):
            tile = keep.tile([P, words.shape[1]], I32, name=name, align_bytes=64)
            nc.sync.dma_start(tile[:], words.rearrange("p c i -> p (c i)").bitcast(I32))
            return tile

        def load_block(src, row_half, col_half, name):
            tile = keep.tile([P, PACK, PASS], F32, name=name)
            block = src[PASS * row_half : PASS * (row_half + 1), PASS * col_half : PASS * (col_half + 1)]
            nc.sync.dma_start(tile[:], block.rearrange("(p i) c -> p i c", i=PACK))
            return tile

        def load_gain(src, name):
            tile = keep.tile([P, 2, PACK], F32, name=name)
            nc.sync.dma_start(tile[:], src.rearrange("(b p t) -> p b t", p=P, t=PACK))
            return tile

        def load_plain(src, name):
            tile = keep.tile([P, src.shape[1]], F32, name=name)
            nc.sync.dma_start(tile[:], src)
            return tile

        tab_plane = zeroed_plane(T, "tab_plane")
        w2_plane_in = zeroed_plane(H, "w2_plane_in")
        tab2_plane = zeroed_plane(T, "tab2_plane")
        w4_plane = zeroed_plane(N, "w4_plane")
        ident = keep.tile([P, P], F32, name="ident")
        make_identity(nc, ident[:])

        idx = load_list(offs, "idx")
        tab_w = [load_words(tab_words[0], "tab_w0")]
        load_plane(tab_plane, tab_scales)
        tab_w.append(load_words(tab_words[1], "tab_w1"))
        w1_rows = {(a, 0): load_block(w1, a, 0, "w1_rows%d0" % a) for a in range(2)}
        load_plane(w2_plane_in, w2_scales)
        w1_rows[0, 1] = load_block(w1, 0, 1, "w1_rows01")
        w2_in = keep.tile([P, 2 * H], U8, name="w2_in", align_bytes=64)
        nc.sync.dma_start(w2_in[:].bitcast(I32), w2_words[0].bitcast(I32))
        idx2 = load_list(offs2, "idx2")
        load_plane(tab2_plane, tab2_scales)
        w1_rows[1, 1] = load_block(w1, 1, 1, "w1_rows11")
        oldest = load_list(pos1, "oldest")
        tab2_w = load_words(tab2_words[0], "tab2_w")
        g2 = load_gain(gain2, "g2")
        g1 = load_gain(gain1, "g1")
        base_rows = {(b, 0): load_block(base, b, 0, "base_rows%d0" % b) for b in range(2)}
        w3_rows = [load_block(w3, b, 0, "w3_rows%d" % b) for b in range(2)]
        base_rows[0, 1] = load_block(base, 0, 1, "base_rows01")
        w4_w = [load_words(w4_words[b], "w4_w%d" % b) for b in range(2)]
        load_plane(w4_plane, w4_scales)
        idx4 = load_list(offs4, "idx4")
        wg2_sb = load_plain(wg2, "wg2_sb")
        pages = [load_plain(page1[n * P : (n + 1) * P, :], "page%d" % n) for n in range(N // P)]
        idx3 = load_list(offs3, "idx3")
        wg1_sb = load_plain(wg1, "wg1_sb")

        stage = [keep.tile([P, 2 * FLEETS], F32, name="stage%d" % i, align_bytes=64) for i in range(2)]
        slices = [keep.tile([P, PACK, FLEETS], BF16, name="slices%d" % b) for b in range(2)]


        def gather(window, offsets, dtype, name):
            picked = keep.tile([P, GROUP * offsets.shape[1]], dtype, name=name, align_bytes=64)
            nc.vector.tensor_copy(picked[:], window.indirect(offsets[:]))
            return picked

        def quantise(src, pool, name, bufs):
            width = src.shape[1] // PACK
            codes = pool.tile([P, width], U32, name=name + "_codes", bufs=bufs, align_bytes=64)
            plane = pool.tile([P, width], U8, name=name + "_plane", bufs=bufs, align_bytes=64)
            nc.vector.quantize_mx(out=codes[:].bitcast(FP8X4), scales=plane[:], in_=src)
            return codes, plane

        def quantise_w1(a, b):
            if (a, b) == (1, 1):
                rounded = keep.tile([P, PACK * PASS], BF16, name="w1_last", tag="v2_w", align_bytes=64)[:]
            else:
                rounded = stage[a][:].bitcast(BF16)
            if a == 0:
                nc.scalar.copy(
                    rounded.rearrange("p (t m i) -> p m t i", t=PACK, i=PACK),
                    w1_rows[a, b][:].rearrange("p i (m t) -> p m t i", t=PACK),
                )
            else:
                nc.vector.tensor_copy(
                    rounded.rearrange("p (u e m i) -> p u m e i", u=2, e=2, i=PACK),
                    w1_rows[a, b][:].rearrange("p i (m u e) -> p u m e i", u=2, e=2),
                )
            return quantise(rounded, keep, "w1q%d%d" % (a, b), 1)

        def quantise_w3(b):
            rounded = stage[b][:].bitcast(BF16)
            nc.vector.tensor_copy(
                rounded.rearrange("p (c e i) -> p c i e", e=4, i=PACK),
                w3_rows[b][:].rearrange("p i (c e) -> p c i e", e=4),
            )
            return quantise(rounded, keep, "w3q%d" % b, 1)

        v_w = [gather(tab_w[0][:].bitcast(U32), idx, U32, "v_w0")]
        v_plane = gather(tab_plane[:], idx, U8, "v_plane")
        v_w.append(gather(tab_w[1][:].bitcast(U32), idx, U32, "v_w1"))

        w2_w = keep.tile([P, 2 * H], U8, name="w2_w", align_bytes=64)
        nc.vector.tensor_copy(
            w2_w[:].bitcast(U16).rearrange("p (b t m) -> p b t m", b=2, t=PACK),
            w2_in[:].bitcast(U16).rearrange("p (b m t) -> p b t m", b=2, t=PACK),
        )
        w2_plane = keep.tile([P, H], U8, name="w2_plane", align_bytes=64)
        nc.vector.tensor_copy(
            w2_plane[:].rearrange("p (b t m) -> p b t m", b=2, t=PACK),
            w2_plane_in[:].rearrange("p (b m t) -> p b t m", b=2, t=PACK),
        )

        w1q = [[quantise_w1(a, 0) for a in range(2)]]
        v2_plane = gather(tab2_plane[:], idx2, U8, "v2_plane")
        w1q.append([quantise_w1(a, 1) for a in range(2)])


        h1_pairs = {}

        def h1_slice(b, t):
            return h1_pairs[b, t // 2][:, t % 2, :]

        for b in range(2):
            for t in range(PACK):
                if t % 2 == 0:
                    h1_pairs[b, t // 2] = keep.tile(
                        [P, 2, S], F32, name="h1_%d%d" % (b, t), tag="w1_rows%d%d" % H1_BUFFER[b, t // 2]
                    )
                rcols = slice(P * t, P * (t + 1))
                for jh in range(2):
                    jcols = slice(PASS * jh, PASS * (jh + 1))
                    bank = banks[H1_BANKS[b][(2 * t + jh) % len(H1_BANKS[b])]]
                    for a in range(2):
                        codes, plane = w1q[b][a]
                        nc.tensor.matmul_mx(
                            out=bank[:],
                            lhsT=codes[:, rcols].bitcast(FP8X4),
                            lhsT_scale=plane[:, rcols],
                            rhs=v_w[a][:, jcols].bitcast(FP8X4),
                            rhs_scale=v_plane[4 * a : P, jcols],
                            start=(a == 0),
                            stop=(a == 1),
                        )
                    nc.scalar.copy(h1_slice(b, t)[:, jcols], bank[:])

        v2_w = gather(tab2_w[:].bitcast(U32), idx2, U32, "v2_w")


        def new_z():
            return work.tile([P, 2, CHUNK, PACK], BF16, name="z", align_bytes=64)

        def interleave(z, b, rows):
            nc.scalar.copy(
                z[:, b].rearrange("p (c e) t -> p c t e", e=4),
                rows.rearrange("p t (c e) -> p c t e", e=4),
            )

        def quantise_z(z):
            return quantise(z[:].rearrange("p b j t -> p (b j t)"), work, "zq", 3)

        def is_added(c, b):
            return b == 0 and c >= FIRST_ADDED

        def added(c):
            return sum_buffers[c].rearrange("p (t j) -> p t j", t=PACK)

        transposed_tanh = {}

        def tanh_ahead(c, b, s):
            given = base_rows[b, c // 2]
            j0, jj = CHUNK * c, CHUNK * (c % 2)
            if not is_added(c, b):
                bank = banks[SUM_BANKS[s]][:].rearrange("p (t j) -> p t j", t=PACK)
                for t in range(PACK):
                    terms = (h1_slice(b, t)[:, j0 + P * s : j0 + P * (s + 1)], given[:, t, jj + P * s : jj + P * (s + 1)])
                    for e, term in enumerate(terms):
                        nc.tensor.matmul(
                            bank[:, t, :], lhsT=term, rhs=ident[:], start=(e == 0), stop=(e == 1), is_transpose=True
                        )
                tanh = work.tile([P, PACK, P], F32, name="tanh", bufs=6)
                nc.scalar.activation(tanh[:], bank, ACT.Tanh)
                transposed_tanh[c, b, s] = tanh
            elif s == 0:
                for u in range(2):
                    nc.vector.tensor_tensor(
                        added(c)[:, 2 * u : 2 * u + 2, :],
                        h1_pairs[b, u][:, :, j0 : j0 + CHUNK],
                        given[:, 2 * u : 2 * u + 2, jj : jj + CHUNK],
                        ALU.add,
                    )
                nc.scalar.activation(added(c), added(c), ACT.Tanh)

        def fleet_slices(b):
            for t in range(PACK):
                picked = stage[t // 2][:, FLEETS * (t % 2) : FLEETS * (t % 2 + 1)]
                nc.vector.tensor_copy(picked, h1_slice(b, t).indirect(oldest[:]))
                bank = banks[PACK * b + t]
                col = PASS * b + P * t
                nc.tensor.matmul_mx(
                    out=bank[:],
                    lhsT=w2_w[:, 2 * col : 2 * (col + P)].bitcast(FP4X4),
                    lhsT_scale=w2_plane[:, col : col + P],
                    rhs=v2_w[:].bitcast(FP8X4),
                    rhs_scale=v2_plane[:],
                    start=True,
                    stop=True,
                )
                least = work.tile([P, FLEETS], F32, name="least", bufs=PACK)
                nc.vector.tensor_tensor(least[:], bank[:], picked, ALU.min)
                nc.scalar.activation(slices[b][:, t, :], least[:], ACT.Copy, scale=g2[:, b, t : t + 1])
                if b == 0:
                    tanh_ahead(0, t // 2, t % 2)

        turns = []

        def vessel_half(z, c, b):
            rounded = slices[b][:, :, CHUNK * (c % 2) : CHUNK * (c % 2 + 1)]
            if is_added(c, b):
                for t in range(PACK):
                    nc.scalar.activation(rounded[:, t, :], added(c)[:, t, :], ACT.Copy, scale=g1[:, b, t : t + 1])
            else:
                turns.append(TURN_BANKS[len(turns) % 2])
                for u in range(2):
                    bank = banks[turns[-1][u]][:].rearrange("p (e j) -> p e j", e=2)
                    for e in range(2):
                        for s in range(2):
                            nc.tensor.transpose(
                                bank[:, e, P * s : P * (s + 1)], transposed_tanh[c, b, s][:, 2 * u + e, :], ident[:]
                            )
                    for e in range(2):
                        t = 2 * u + e
                        nc.scalar.activation(rounded[:, t, :], bank[:, e, :], ACT.Copy, scale=g1[:, b, t : t + 1])
            if c + 1 < CHUNKS:
                tanh_ahead(c + 1, b, 0)
            interleave(z, b, rounded)
            if c + 1 < CHUNKS:
                tanh_ahead(c + 1, b, 1)


        def new_y(count):
            return work.tile([P, 2, CHUNK], F32, name="y", bufs=4)[:, 0:count, :]

        def product(bank, weights, parts, y):
            for e, (n, (codes, plane)) in enumerate(parts):
                ncols = slice(P * n, P * (n + 1))
                for b in range(2):
                    wcodes, wplane = weights[b]
                    nc.tensor.matmul_mx(
                        out=bank[:, CHUNK * e : CHUNK * (e + 1)],
                        lhsT=wcodes[:, ncols].bitcast(FP8X4),
                        lhsT_scale=wplane[:, ncols],
                        rhs=codes[:, CHUNK * b : CHUNK * (b + 1)].bitcast(FP8X4),
                        rhs_scale=plane[:, CHUNK * b : CHUNK * (b + 1)],
                        start=(b == 0),
                        stop=(b == 1),
                    )
            nc.scalar.copy(y, bank[:, 0 : CHUNK * len(parts)].rearrange("p (e j) -> p e j", j=CHUNK))

        def scatter(n, values, offsets, factors, j0, count):
            nc.vector.tensor_tensor(
                pages[n][:].indirect(offsets[:, j0 // GROUP : (j0 + count) // GROUP]),
                values,
                factors[:, j0 : j0 + count],
                ALU.mult,
            )

        def place_fleets(bank, n):
            y = new_y(2)
            product(banks[bank], w4q, [(n, zq) for zq in zq_fleets], y)
            scatter(n, y.rearrange("p e j -> p (e j)"), idx4, wg2_sb, 0, FLEETS)

        def place_vessels(bank, c, u, y):
            product(banks[bank], w3q, [(2 * u, zq_vessels[c]), (2 * u + 1, zq_vessels[c])], y)
            for e in range(2):
                scatter(2 * u + e, y[:, e, :], idx3, wg1_sb, CHUNK * c, CHUNK)

        def store(n):
            nc.sync.dma_start(out[P * n : P * (n + 1), :], pages[n][:])

        z_fleets = [new_z() for c in range(2)]
        w4q = [(w4_w[b], w4_plane[4 * b : P, :]) for b in range(2)]
        fleet_slices(0)
        for c in range(2):
            interleave(z_fleets[c], 0, slices[0][:, :, CHUNK * c : CHUNK * (c + 1)])
        fleet_slices(1)
        w3q = [quantise_w3(b) for b in range(2)]
        base_rows[1, 1] = load_block(base, 1, 1, "w3_rows0")
        last_sum = keep.tile([P, PACK * CHUNK], F32, name="last_sum", tag="w3_rows1")
        sum_buffers = {1: stage[1][:], 2: stage[0][:], 3: last_sum[:]}
        zq_fleets = []
        for c in range(2):
            interleave(z_fleets[c], 1, slices[1][:, :, CHUNK * c : CHUNK * (c + 1)])
            zq_fleets.append(quantise_z(z_fleets[c]))
        for n in range(2):
            place_fleets(SPARE_BANKS[n], n)

        zq_vessels = []
        for c in range(CHUNKS):
            z = new_z()
            vessel_half(z, c, 0)
            if c == 0:
                place_fleets(turns[-1][1], 2)
            else:
                place_vessels(SPARE_BANKS[0], c - 1, 0, added(c)[:, 2:4, :])
            vessel_half(z, c, 1)
            zq_vessels.append(quantise_z(z))
            if c == 0:
                place_fleets(turns[-1][1], 3)
            elif c + 1 < CHUNKS:
                place_vessels(turns[-1][1], c - 1, 1, new_y(2))

        before, last = CHUNKS - 2, CHUNKS - 1
        y = new_y(1)
        product(banks[turns[-1][1]], w3q, [(2, zq_vessels[before])], y)
        scatter(2, y[:, 0, :], idx3, wg1_sb, CHUNK * before, CHUNK)
        place_vessels(SPARE_BANKS[0], last, 0, new_y(2))
        store(0)
        store(1)
        y = new_y(1)
        product(banks[SPARE_BANKS[1]], w3q, [(2, zq_vessels[last])], y)
        scatter(2, y[:, 0, :], idx3, wg1_sb, CHUNK * last, CHUNK)
        store(2)
        y = new_y(2)
        product(banks[SUM_BANKS[0]], w3q, [(3, zq_vessels[before]), (3, zq_vessels[last])], y)
        scatter(3, y.rearrange("p e j -> p (e j)"), idx3, wg1_sb, CHUNK * before, 2 * CHUNK)
        store(3)
